import numpy as np
import ml_dtypes


def mxq(x, axis, fmt="e4m3"):
    dtype, down = {"e4m3": (ml_dtypes.float8_e4m3fn, 7), "e5m2": (ml_dtypes.float8_e5m2, 14)}[fmt]
    v = np.moveaxis(np.asarray(x, np.float32).astype(ml_dtypes.bfloat16).astype(np.float64), axis, -1)
    blocks = v.reshape(v.shape[:-1] + (-1, 32))
    amax = np.abs(blocks).max(-1, keepdims=True)
    byte = np.maximum(np.where(amax > 0, np.frexp(amax)[1] - 1 + 127, 0) - down, 1)
    scale = np.exp2(byte - 127.0)
    codes = (blocks / scale).astype(np.float32).astype(dtype).astype(np.float64)
    return np.moveaxis((codes * scale).reshape(v.shape), -1, axis)


WIDE = False


def mx_kscale(k):
    if not WIDE:
        return np.ones(k)
    levels = np.array([10, -10, 5, -5, 0])
    if k % 512:
        return np.exp2(np.random.permutation(np.resize(levels, k // 32))).repeat(32)
    a = np.empty((k // 512, 16))
    for p in range(k // 512):
        a[p, :8] = np.random.permutation(np.resize(levels, 8))
        for g in range(8):
            far = levels[np.abs(levels - a[p, g]) >= 10]
            a[p, g + 8] = far[np.random.randint(len(far))]
    return np.exp2(a.ravel()).repeat(32)


def f64(x):
    return np.asarray(x).astype(np.float64)


def striped(idx):
    return np.tile(idx.reshape(-1, 16).T, (8, 1)).astype(np.uint16)


def unstriped(offs):
    return offs[:16].T.reshape(-1).astype(np.int64)


E2M1 = np.array([0.0, 0.5, 1.0, 1.5, 2.0, 3.0, 4.0, 6.0, -0.0, -0.5, -1.0, -1.5, -2.0, -3.0, -4.0, -6.0])


def pack_weight(w, fmt):
    k, n = w.shape
    w = f64(np.asarray(w, np.float32).astype(ml_dtypes.bfloat16)).reshape(k // 32, 32, n)
    amax = np.abs(w).max(1)
    if fmt == "e4m3":
        byte = np.frexp(amax)[1] - 1 + 127 - 7
    else:
        mant, ex = np.frexp(amax / 6.0)
        byte = np.where(mant > 0.5, ex, ex - 1) + 127
    byte = np.clip(np.where(amax > 0, byte, 1), 1, 254)
    scaled = (w * np.exp2(127.0 - byte)[:, None, :]).reshape(k, n).astype(np.float32)
    by_word = np.ascontiguousarray(scaled.reshape(k // 512, 128, 4, n).transpose(0, 1, 3, 2))
    if fmt == "e4m3":
        words = by_word.astype(ml_dtypes.float8_e4m3fn).view(np.uint8)
    else:
        c = by_word.astype(ml_dtypes.float4_e2m1fn).view(np.uint8) & 0xF
        words = (c[..., 0::2] | (c[..., 1::2] << 4)).reshape(k // 512, 128, 2 * n)
    return np.ascontiguousarray(words), np.ascontiguousarray(byte.astype(np.uint8).reshape(k // 512, 16, n))


def unpack_weight(words, scales, fmt):
    g, _, n = scales.shape
    words = np.ascontiguousarray(words).reshape(g, 128, n, -1)
    if fmt == "e4m3":
        vals = words.view(ml_dtypes.float8_e4m3fn).astype(np.float64)
    else:
        nib = np.empty((g, 128, n, 4), np.uint8)
        nib[..., 0::2] = words & 0xF
        nib[..., 1::2] = words >> 4
        vals = E2M1[nib]
    vals = vals * np.repeat(np.exp2(scales.astype(np.float64) - 127.0), 8, axis=1)[..., None]
    return vals.transpose(0, 1, 3, 2).reshape(g * 512, n)


def gelu(v):
    return 0.5 * v * (1.0 + np.tanh(np.sqrt(2.0 / np.pi) * (v + 0.044715 * v**3)))


def bf(x):
    return np.asarray(x, np.float32).astype(ml_dtypes.bfloat16)


def planes(Y):
    n, m = Y.shape
    b = f64(bf(Y)).reshape(n // 32, 32, m)
    amax = np.abs(b).max(1)
    byte = np.clip(np.where(amax > 0, np.frexp(amax)[1] - 1 + 127 - 7, 1), 1, 254)
    codes = (b * np.exp2(127.0 - byte)[:, None, :]).reshape(n, m).astype(np.float32).astype(ml_dtypes.float8_e4m3fn).view(np.uint8)
    words = codes.reshape(n // 512, 128, 4, m).transpose(0, 1, 3, 2)
    return np.ascontiguousarray(words), np.ascontiguousarray(byte.astype(np.uint8).reshape(n // 512, 16, m))


K, T, S, H, N = 1024, 2048, 1024, 512, 384


def setup_inputs():
    n = np.random.standard_normal
    s = mx_kscale(K)[:, None]
    u = mx_kscale(H)[:, None]
    busy = n((K, H)) / np.sqrt(K) / s
    idle = n((K, H)) / np.sqrt(K) / s
    tab_words, tab_scales = pack_weight(n((K, T)) * s, "e4m3")
    w8_words, w8_scales = pack_weight(idle * u.T, "e4m3")
    w4_words, w4_scales = pack_weight(busy + idle, "e2m1")
    return {
        "tab_words": tab_words, "tab_scales": tab_scales,
        "offs": striped(np.random.permutation(T)[:S]),
        "w1": (busy * u.T).astype(np.float32),
        "w8_words": w8_words, "w8_scales": w8_scales,
        "w4_words": w4_words, "w4_scales": w4_scales,
        "level": np.random.uniform(0.5, 1.5, H).astype(np.float32),
        "wg": (1.5 * n((H, N)) / np.sqrt(H) / u).astype(np.float32),
        "wr": (n((K, N)) / np.sqrt(K) / s).astype(np.float32),
    }


def reference(tab_words, tab_scales, offs, w1, w8_words, w8_scales, w4_words, w4_scales, level, wg, wr):
    v = unpack_weight(tab_words, tab_scales, "e4m3")[:, unstriped(offs)]
    a = mxq(f64(w1), 0, "e4m3").T @ v
    b = unpack_weight(w8_words, w8_scales, "e4m3").T @ v
    both = unpack_weight(w4_words, w4_scales, "e2m1").T @ v
    h = (a - b) / (np.abs(both) + f64(level)[:, None])
    words, scales = planes(h)
    gate = mxq(f64(wg), 0, "e4m3").T @ mxq(h, 0, "e4m3")
    raw = mxq(f64(wr), 0, "e4m3").T @ v
    y = raw / (1.0 + np.exp(-gate))
    return y, h, words, scales

@@ -1,0 +1,330 @@
+from contextlib import ExitStack
+
+import concourse.mybir as mybir
+
+K, T, S, H, N = 1024, 2048, 1024, 512, 384
+FLOPS = 2 * S * (3 * K * H + K * N + H * N)
+
+F32 = mybir.dt.float32
+BF16 = mybir.dt.bfloat16
+I32 = mybir.dt.int32
+U32 = mybir.dt.uint32
+U16 = mybir.dt.uint16
+U8 = mybir.dt.uint8
+FP8X4 = mybir.dt.float8_e4m3fn_x4
+FP4X4 = mybir.dt.float4_e2m1fn_x4
+ACT = mybir.ActivationFunctionType
+ALU = mybir.AluOpType
+
+P = 128
+PACK = 4
+KP = P * PACK
+PASSES = K // KP
+CH = 512
+CHUNKS = S // CH
+NT = N // P
+
+
+def tile_list_spectrum_probe_contrast_kernel(
+    tc, tab_words, tab_scales, offs, w1, w8_words, w8_scales, w4_words, w4_scales, level, wg, wr,
+    out_0, out_1, out_2, out_3,
+):
+    nc = tc.nc
+    with ExitStack() as ctx:
+        keep = ctx.enter_context(tc.tile_pool(name="keep", bufs=1))
+        turns = ctx.enter_context(tc.tile_pool(name="turns", bufs=1))
+        ring = ctx.enter_context(tc.tile_pool(name="ring", bufs=3))
+        psa = ctx.enter_context(tc.psum_pool(name="psa", bufs=3))
+        psb = ctx.enter_context(tc.psum_pool(name="psb", bufs=5))
+
+        offsets = keep.tile([P, S // 16], U16, name="offsets")
+        tsc = turns.tile([P, T], U8, name="tsc", align_bytes=64, offset=4096)
+        wsc = keep.tile([P, PASSES * H], U8, name="wsc", align_bytes=64)
+        vs1 = keep.tile([P, S], U8, name="vs1", align_bytes=64)
+        warm = keep.tile([P, 1], F32, name="warm")
+        warm2 = keep.tile([P, 1], F32, name="warm2")
+        w8sc = turns.tile([P, H], U8, name="w8sc", align_bytes=64, offset=4224)
+        vs = keep.tile([P, S], U8, name="vs", align_bytes=64)
+        for q in range(4):
+            nc.vector.memset(tsc[32 * q:32 * q + 24, :].bitcast(I32), 0)
+        nc.gpsimd.memset(wsc[:].bitcast(I32), 0)
+        nc.gpsimd.memset(warm[:], 1.0)
+        nc.gpsimd.memset(vs[:].bitcast(I32), 0)
+        nc.gpsimd.memset(vs1[:].bitcast(I32), 0)
+        nc.scalar.activation(out=warm2[:], in_=warm[:], func=ACT.Abs_reciprocal_sqrt)
+
+        nc.sync.dma_start(offsets[:], offs)
+        tabw = [turns.tile([P, T], I32, name=f"tabw{a}", align_bytes=64, offset=(20480, 36864)[a]) for a in range(PASSES)]
+        w1raw = [turns.tile([P, PACK * H], F32, name=f"w1raw{a}", align_bytes=64, offset=(28672, 6080)[a]) for a in range(PASSES)]
+        wrraw = [turns.tile([P, PACK * N], F32, name=f"wrraw{a}", align_bytes=64, offset=(14336, 20480)[a]) for a in range(PASSES)]
+        wgraw = turns.tile([P, PACK * N], F32, name="wgraw", align_bytes=64, offset=28672)
+        w4raw = turns.tile([P, PASSES * 2 * H], U8, name="w4raw", align_bytes=64, offset=14336)
+        w8raw = turns.tile([P, PASSES * H], I32, name="w8raw", align_bytes=64, offset=64)
+        lev = turns.tile([P, PACK], F32, name="lev", align_bytes=64, offset=4160)
+
+        def load_tab(a):
+            nc.sync.dma_start(tabw[a][:], tab_words[a].rearrange("p t i -> p (t i)").bitcast(I32))
+
+        def load_rows(dst, src, a):
+            nc.sync.dma_start(dst[:], src[a * KP:(a + 1) * KP, :].rearrange("(p j) c -> p (j c)", j=PACK))
+
+        def load_wscales(eng, src, row0):
+            for q in range(4):
+                eng.dma_start(
+                    wsc[32 * q + row0:32 * q + row0 + 4, :].bitcast(I32).rearrange("r (a c) -> r a c", a=PASSES),
+                    src[:, 4 * q:4 * q + 4, :].bitcast(I32).rearrange("a r c -> r a c"),
+                )
+
+        for q in range(4):
+            nc.sync.dma_start(tsc[32 * q + 24:32 * q + 32, :].bitcast(I32), tab_scales[:, 4 * q:4 * q + 4, :].bitcast(I32))
+        nc.sync.dma_start(
+            w4raw[:].bitcast(I32).rearrange("p (a c) -> p a c", a=PASSES),
+            w4_words.bitcast(I32).rearrange("a p c -> p a c"),
+        )
+        load_tab(0)
+        load_rows(w1raw[0], w1, 0)
+        load_wscales(nc.sync, w4_scales, 0)
+        load_tab(1)
+
+        vsg = keep.tile([P, S], U8, name="vsg", align_bytes=64)
+        nc.vector.tensor_copy(vsg[:], tsc[:].indirect(offsets[:]))
+        nc.scalar.dma_start(vs[0:104, :].bitcast(I32), vsg[24:128, :].bitcast(I32))
+        nc.scalar.dma_start(vs1[0:100, :].bitcast(I32), vsg[28:128, :].bitcast(I32))
+
+        nc.gpsimd.memset(w8sc[:].bitcast(I32), 0)
+        nc.sync.dma_start(lev[:], level.rearrange("(p t) -> p t", t=PACK))
+        nc.sync.dma_start(
+            w8raw[:].rearrange("p (a c) -> p a c", a=PASSES),
+            w8_words.rearrange("a p c i -> p a (c i)").bitcast(I32),
+        )
+        load_rows(w1raw[1], w1, 1)
+        for q in range(4):
+            nc.sync.dma_start(w8sc[32 * q:32 * q + 8, :].bitcast(I32), w8_scales[:, 4 * q:4 * q + 4, :].bitcast(I32))
+
+        w4p = keep.tile([P, PASSES * 2 * H], U8, name="w4p", align_bytes=64)
+        nc.vector.tensor_copy(
+            w4p[:].rearrange("p (a t m b) -> p a t m b", a=PASSES, t=PACK, b=2),
+            w4raw[:].rearrange("p (a m t b) -> p a t m b", a=PASSES, t=PACK, b=2),
+        )
+        load_rows(wrraw[0], wr, 0)
+        wscp = turns.tile([P, PASSES * H], U8, name="wscp", align_bytes=64, offset=26624)
+        w8scp = turns.tile([P, H], U8, name="w8scp", align_bytes=64, offset=40960)
+
+        def deal_w4_scales():
+            nc.vector.tensor_copy(
+                wscp[:].rearrange("p (a t m) -> p a t m", a=PASSES, t=PACK),
+                wsc[:].rearrange("p (a m t) -> p a t m", a=PASSES, t=PACK),
+            )
+
+        def deal_w8():
+            nc.vector.tensor_copy(
+                w8p[:].rearrange("p (a t m) -> p a m t", a=PASSES, t=PACK),
+                w8raw[:].rearrange("p (a m t) -> p a m t", a=PASSES, t=PACK),
+            )
+            nc.vector.tensor_copy(
+                w8scp[:].rearrange("p (t m) -> p t m", t=PACK),
+                w8sc[:].rearrange("p (m t) -> p t m", t=PACK),
+            )
+
+        vw = [[keep.tile([P, CH], U32, name=f"vw{a}_{c}", align_bytes=64) for c in range(CHUNKS)] for a in range(PASSES)]
+
+        def gather(a, c):
+            cols = slice(c * (CH // 16), (c + 1) * (CH // 16))
+            nc.vector.tensor_copy(vw[a][c][:], tabw[a][:].bitcast(U32).indirect(offsets[:, cols]))
+
+        w1bf = [keep.tile([P, PACK * H], BF16, name=f"w1bf{a}", align_bytes=64) for a in range(PASSES)]
+        w1q = [turns.tile([P, H], U32, name=f"w1q{a}", align_bytes=64, offset=(41472, 45056)[a]) for a in range(PASSES)]
+        w1s = [keep.tile([P, H], U8, name=f"w1s{a}", align_bytes=64) for a in range(PASSES)]
+
+        def cast_w1(a, on_scalar):
+            dst = w1bf[a][:].rearrange("p (t m j) -> p m j t", t=PACK, j=PACK)
+            src = w1raw[a][:].rearrange("p (j m t) -> p m j t", t=PACK, j=PACK)
+            if on_scalar:
+                nc.scalar.activation(out=dst, in_=src, func=ACT.Copy, scale=-1.0)
+            else:
+                nc.vector.tensor_scalar(dst, src, -1.0, None, ALU.mult)
+
+        def quant_w1(a):
+            nc.vector.quantize_mx(out=w1q[a][:].bitcast(FP8X4), scales=w1s[a][:], in_=w1bf[a][:])
+
+        def vscale(a, c):
+            return vs[4 * a:, c * CH:(c + 1) * CH]
+
+        recip = {}
+        mags = {}
+
+        def both(c, t):
+            acc = psa.tile([P, CH], F32, name="acc_s")
+            for a in range(PASSES):
+                col = a * H + t * P
+                plane = vs if a == 0 else vs1
+                nc.tensor.matmul_mx(
+                    out=acc[:],
+                    lhsT=w4p[:, 2 * col:2 * (col + P)].bitcast(FP4X4), lhsT_scale=wscp[:, col:col + P],
+                    rhs=vw[a][c][:].bitcast(FP8X4), rhs_scale=plane[:, c * CH:(c + 1) * CH],
+                    start=(a == 0), stop=(a == PASSES - 1),
+                )
+            mags[c, t] = keep.tile([P, CH], F32, name=f"mag{c}_{t}")
+            nc.scalar.activation(out=mags[c, t][:], in_=acc[:], func=ACT.Abs)
+
+        def invert(c, t):
+            root = ring.tile([P, CH], F32, name="root")
+            nc.scalar.activation(out=root[:], in_=mags[c, t][:], func=ACT.Abs_reciprocal_sqrt, bias=lev[:, t:t + 1])
+            recip[c, t] = keep.tile([P, CH], F32, name=f"recip{c}_{t}")
+            nc.scalar.activation(out=recip[c, t][:], in_=root[:], func=ACT.Square)
+
+        w8p = turns.tile([P, PASSES * H], I32, name="w8p", align_bytes=64, offset=36864)
+        hs = [keep.tile([P, PACK, CH], F32, name=f"h{c}", align_bytes=64) for c in range(CHUNKS)]
+        out1v = out_1.rearrange("(p t) s -> p t s", t=PACK)
+
+        diff = {}
+
+        def w1_pass(c, t, a, start, stop):
+            nc.tensor.matmul_mx(
+                out=diff[c, t][:],
+                lhsT=w1q[a][:, t * P:(t + 1) * P].bitcast(FP8X4), lhsT_scale=w1s[a][:, t * P:(t + 1) * P],
+                rhs=vw[a][c][:].bitcast(FP8X4), rhs_scale=vscale(a, c),
+                start=start, stop=stop,
+            )
+
+        def open_diff(c, t):
+            diff[c, t] = psb.tile([P, CH], F32, name="acc_v")
+            w1_pass(c, t, 0, True, False)
+
+        def w8_passes(c, t):
+            for a in range(PASSES):
+                col = a * H + t * P
+                nc.tensor.matmul_mx(
+                    out=diff[c, t][:],
+                    lhsT=w8p[:, col:col + P].bitcast(FP8X4), lhsT_scale=w8scp[4 * a:, t * P:(t + 1) * P],
+                    rhs=vw[a][c][:].bitcast(FP8X4), rhs_scale=vscale(a, c),
+                    start=False, stop=False,
+                )
+
+        def close_diff(c, t):
+            w1_pass(c, t, 1, False, True)
+            nc.vector.scalar_tensor_tensor(hs[c][:, t, :], diff[c, t][:], -1.0, recip[c, t][:], ALU.mult, ALU.mult)
+            nc.sync.dma_start(out1v[:, t, c * CH:(c + 1) * CH], hs[c][:, t, :])
+
+        obf = keep.tile([P, (PASSES + 1) * N * PACK], BF16, name="obf", align_bytes=64)
+        oq = keep.tile([P, (PASSES + 1) * N], U32, name="oq", align_bytes=64)
+        osc = keep.tile([P, (PASSES + 1) * N], U8, name="osc", align_bytes=64)
+
+        def cast_o(src, slot, on_scalar=False):
+            dst = obf[:, slot * N * PACK:(slot + 1) * N * PACK].rearrange("p (c i j) -> p c j i", i=4, j=PACK)
+            view = src[:].rearrange("p (j c i) -> p c j i", i=4, j=PACK)
+            if on_scalar:
+                nc.scalar.activation(out=dst, in_=view, func=ACT.Copy)
+            else:
+                nc.vector.tensor_copy(dst, view)
+
+        def quant_o(lo, hi):
+            nc.vector.quantize_mx(out=oq[:, lo:hi].bitcast(FP8X4), scales=osc[:, lo:hi], in_=obf[:, PACK * lo:PACK * hi])
+
+        hq = keep.tile([P, S], U32, name="hq", align_bytes=64)
+        hsc = keep.tile([P, S], U8, name="hsc", align_bytes=64)
+        out2v = out_2[0].rearrange("p s i -> p (s i)").bitcast(I32)
+
+        hbf = [keep.tile([P, CH * PACK], BF16, name=f"hbf{c}", align_bytes=64) for c in range(CHUNKS)]
+
+        def cast_h(c):
+            nc.vector.tensor_copy(
+                hbf[c][:].rearrange("p (c i t) -> p c t i", i=4, t=PACK),
+                hs[c][:].rearrange("p t (c i) -> p c t i", i=4),
+            )
+
+        def quant_h(c):
+            cols = slice(c * CH, (c + 1) * CH)
+            nc.vector.quantize_mx(out=hq[:, cols].bitcast(FP8X4), scales=hsc[:, cols], in_=hbf[c][:])
+            nc.sync.dma_start(out2v[:, cols], hq[:, cols].bitcast(I32))
+
+        raws = {}
+
+        def raw_product(c, j):
+            raws[c, j] = psb.tile([P, CH], F32, name="acc_v")
+            for a in range(PASSES):
+                col = a * N + j * P
+                nc.tensor.matmul_mx(
+                    out=raws[c, j][:],
+                    lhsT=oq[:, col:col + P].bitcast(FP8X4), lhsT_scale=osc[:, col:col + P],
+                    rhs=vw[a][c][:].bitcast(FP8X4), rhs_scale=vscale(a, c),
+                    start=(a == 0), stop=(a == PASSES - 1),
+                )
+
+        def readout(c, j):
+            cols = slice(c * CH, (c + 1) * CH)
+            gate = psa.tile([P, CH], F32, name="acc_s")
+            col = PASSES * N + j * P
+            nc.tensor.matmul_mx(
+                out=gate[:],
+                lhsT=oq[:, col:col + P].bitcast(FP8X4), lhsT_scale=osc[:, col:col + P],
+                rhs=hq[:, cols].bitcast(FP8X4), rhs_scale=hsc[:, cols],
+                start=True, stop=True,
+            )
+            sig = ring.tile([P, CH], F32, name="sig")
+            nc.scalar.activation(out=sig[:], in_=gate[:], func=ACT.Sigmoid)
+            y = ring.tile([P, CH], F32, name="y")
+            nc.vector.tensor_tensor(y[:], raws[c, j][:], sig[:], ALU.mult)
+            nc.sync.dma_start(out_0[j * P:(j + 1) * P, cols], y[:])
+
+        gather(0, 0)
+        gather(0, 1)
+        load_rows(wrraw[1], wr, 1)
+        cast_w1(0, True)
+        load_rows(wgraw, wg, 0)
+        deal_w4_scales()
+        gather(1, 0)
+        both(0, 0)
+        both(0, 1)
+        invert(0, 0)
+        both(0, 2)
+        gather(1, 1)
+        quant_w1(0)
+        deal_w8()
+        both(0, 3)
+        invert(0, 1)
+        cast_w1(1, False)
+        for t in range(PACK):
+            open_diff(0, t)
+        both(1, 0)
+        invert(0, 2)
+        quant_w1(1)
+        for t in range(PACK):
+            w8_passes(0, t)
+        both(1, 1)
+        invert(0, 3)
+        close_diff(0, 0)
+        close_diff(0, 1)
+        cast_o(wrraw[0], 0)
+        both(1, 2)
+        invert(1, 0)
+        close_diff(0, 2)
+        close_diff(0, 3)
+        cast_o(wrraw[1], 1)
+        both(1, 3)
+        invert(1, 1)
+        invert(1, 2)
+        invert(1, 3)
+        cast_h(0)
+        quant_o(0, 512)
+        quant_o(512, 768)
+        cast_o(wgraw, 2)
+        quant_h(0)
+        for t in range(PACK):
+            open_diff(1, t)
+            w8_passes(1, t)
+            close_diff(1, t)
+            if t == 0:
+                quant_o(768, 1024)
+                quant_o(1024, 1152)
+        cast_h(1)
+        for j in range(NT):
+            raw_product(0, j)
+        quant_h(1)
+        for j in range(NT):
+            readout(0, j)
+        for q in range(4):
+            nc.sync.dma_start(out_3[0, 4 * q:4 * q + 4, :].bitcast(I32), hsc[32 * q:32 * q + 4, :].bitcast(I32))
+        for j in range(NT):
+            raw_product(1, j)
+            readout(1, j)

@@ -34,33 +34,33 @@ def tile_list_spectrum_probe_contrast_kernel(
         keep = ctx.enter_context(tc.tile_pool(name="keep", bufs=1))
         turns = ctx.enter_context(tc.tile_pool(name="turns", bufs=1))
         ring = ctx.enter_context(tc.tile_pool(name="ring", bufs=3))
-        psa = ctx.enter_context(tc.psum_pool(name="psa", bufs=3))
-        psb = ctx.enter_context(tc.psum_pool(name="psb", bufs=5))
+        psum = ctx.enter_context(tc.psum_pool(name="psum", bufs=1))
 
         offsets = keep.tile([P, S // 16], U16, name="offsets")
-        tsc = turns.tile([P, T], U8, name="tsc", align_bytes=64, offset=4096)
+        tsc = keep.tile([P, T], U8, name="tsc", align_bytes=64)
         wsc = keep.tile([P, PASSES * H], U8, name="wsc", align_bytes=64)
         vs1 = keep.tile([P, S], U8, name="vs1", align_bytes=64)
         warm = keep.tile([P, 1], F32, name="warm")
         warm2 = keep.tile([P, 1], F32, name="warm2")
-        w8sc = turns.tile([P, H], U8, name="w8sc", align_bytes=64, offset=4224)
+        w8sc = keep.tile([P, H], U8, name="w8sc", align_bytes=64)
         vs = keep.tile([P, S], U8, name="vs", align_bytes=64)
         for q in range(4):
             nc.vector.memset(tsc[32 * q:32 * q + 24, :].bitcast(I32), 0)
         nc.gpsimd.memset(wsc[:].bitcast(I32), 0)
         nc.gpsimd.memset(warm[:], 1.0)
-        nc.gpsimd.memset(vs[:].bitcast(I32), 0)
-        nc.gpsimd.memset(vs1[:].bitcast(I32), 0)
+        nc.gpsimd.memset(w8sc[:].bitcast(I32), 0)
+        nc.vector.memset(vs[:].bitcast(I32), 0)
+        nc.vector.memset(vs1[:].bitcast(I32), 0)
         nc.scalar.activation(out=warm2[:], in_=warm[:], func=ACT.Abs_reciprocal_sqrt)
 
         nc.sync.dma_start(offsets[:], offs)
         tabw = [turns.tile([P, T], I32, name=f"tabw{a}", align_bytes=64, offset=(20480, 36864)[a]) for a in range(PASSES)]
         w1raw = [turns.tile([P, PACK * H], F32, name=f"w1raw{a}", align_bytes=64, offset=(28672, 6080)[a]) for a in range(PASSES)]
-        wrraw = [turns.tile([P, PACK * N], F32, name=f"wrraw{a}", align_bytes=64, offset=(14336, 20480)[a]) for a in range(PASSES)]
-        wgraw = turns.tile([P, PACK * N], F32, name="wgraw", align_bytes=64, offset=28672)
-        w4raw = turns.tile([P, PASSES * 2 * H], U8, name="w4raw", align_bytes=64, offset=14336)
+        wrraw = [turns.tile([P, PACK * N], F32, name=f"wrraw{a}", align_bytes=64, offset=(14400, 28672)[a]) for a in range(PASSES)]
+        wgraw = turns.tile([P, PACK * N], F32, name="wgraw", align_bytes=64, offset=43520)
+        w4raw = turns.tile([P, PASSES * 2 * H], U8, name="w4raw", align_bytes=64, offset=4096)
         w8raw = turns.tile([P, PASSES * H], I32, name="w8raw", align_bytes=64, offset=64)
-        lev = turns.tile([P, PACK], F32, name="lev", align_bytes=64, offset=4160)
+        lev = keep.tile([P, PACK], F32, name="lev")
 
         def load_tab(a):
             nc.sync.dma_start(tabw[a][:], tab_words[a].rearrange("p t i -> p (t i)").bitcast(I32))
@@ -81,6 +81,9 @@ def tile_list_spectrum_probe_contrast_kernel(
             w4raw[:].bitcast(I32).rearrange("p (a c) -> p a c", a=PASSES),
             w4_words.bitcast(I32).rearrange("a p c -> p a c"),
         )
+        nc.gpsimd.dma_start(lev[:], level.rearrange("(p t) -> p t", t=PACK))
+        for q in range(4):
+            nc.gpsimd.dma_start(w8sc[32 * q:32 * q + 8, :].bitcast(I32), w8_scales[:, 4 * q:4 * q + 4, :].bitcast(I32))
         load_tab(0)
         load_rows(w1raw[0], w1, 0)
         load_wscales(nc.sync, w4_scales, 0)
@@ -91,22 +94,16 @@ def tile_list_spectrum_probe_contrast_kernel(
         nc.scalar.dma_start(vs[0:104, :].bitcast(I32), vsg[24:128, :].bitcast(I32))
         nc.scalar.dma_start(vs1[0:100, :].bitcast(I32), vsg[28:128, :].bitcast(I32))
 
-        nc.gpsimd.memset(w8sc[:].bitcast(I32), 0)
-        nc.sync.dma_start(lev[:], level.rearrange("(p t) -> p t", t=PACK))
-        nc.sync.dma_start(
-            w8raw[:].rearrange("p (a c) -> p a c", a=PASSES),
-            w8_words.rearrange("a p c i -> p a (c i)").bitcast(I32),
-        )
-        load_rows(w1raw[1], w1, 1)
-        for q in range(4):
-            nc.sync.dma_start(w8sc[32 * q:32 * q + 8, :].bitcast(I32), w8_scales[:, 4 * q:4 * q + 4, :].bitcast(I32))
-
         w4p = keep.tile([P, PASSES * 2 * H], U8, name="w4p", align_bytes=64)
         nc.vector.tensor_copy(
             w4p[:].rearrange("p (a t m b) -> p a t m b", a=PASSES, t=PACK, b=2),
             w4raw[:].rearrange("p (a m t b) -> p a t m b", a=PASSES, t=PACK, b=2),
         )
-        load_rows(wrraw[0], wr, 0)
+        nc.sync.dma_start(
+            w8raw[:].rearrange("p (a c) -> p a c", a=PASSES),
+            w8_words.rearrange("a p c i -> p a (c i)").bitcast(I32),
+        )
+        load_rows(w1raw[1], w1, 1)
         wscp = turns.tile([P, PASSES * H], U8, name="wscp", align_bytes=64, offset=26624)
         w8scp = turns.tile([P, H], U8, name="w8scp", align_bytes=64, offset=40960)
 
@@ -132,8 +129,8 @@ def tile_list_spectrum_probe_contrast_kernel(
             cols = slice(c * (CH // 16), (c + 1) * (CH // 16))
             nc.vector.tensor_copy(vw[a][c][:], tabw[a][:].bitcast(U32).indirect(offsets[:, cols]))
 
-        w1bf = [keep.tile([P, PACK * H], BF16, name=f"w1bf{a}", align_bytes=64) for a in range(PASSES)]
-        w1q = [turns.tile([P, H], U32, name=f"w1q{a}", align_bytes=64, offset=(41472, 45056)[a]) for a in range(PASSES)]
+        w1bf = [keep.tile([P, PACK * H], BF16, name=f"w1bf{a}", tag=f"w1bf{a}", align_bytes=64) for a in range(PASSES)]
+        w1q = [turns.tile([P, H], U32, name=f"w1q{a}", align_bytes=64, offset=(41472, 49664)[a]) for a in range(PASSES)]
         w1s = [keep.tile([P, H], U8, name=f"w1s{a}", align_bytes=64) for a in range(PASSES)]
 
         def cast_w1(a, on_scalar):
@@ -153,8 +150,8 @@ def tile_list_spectrum_probe_contrast_kernel(
         recip = {}
         mags = {}
 
-        def both(c, t):
-            acc = psa.tile([P, CH], F32, name="acc_s")
+        def both(c, t, bank):
+            acc = psum.tile([P, CH], F32, name=f"bank{bank}")
             for a in range(PASSES):
                 col = a * H + t * P
                 plane = vs if a == 0 else vs1
@@ -170,7 +167,7 @@ def tile_list_spectrum_probe_contrast_kernel(
         def invert(c, t):
             root = ring.tile([P, CH], F32, name="root")
             nc.scalar.activation(out=root[:], in_=mags[c, t][:], func=ACT.Abs_reciprocal_sqrt, bias=lev[:, t:t + 1])
-            recip[c, t] = keep.tile([P, CH], F32, name=f"recip{c}_{t}")
+            recip[c, t] = keep.tile([P, CH], F32, name=f"recip{c}_{t}", tag=f"recip{c}_{t}", align_bytes=64)
             nc.scalar.activation(out=recip[c, t][:], in_=root[:], func=ACT.Square)
 
         w8p = turns.tile([P, PASSES * H], I32, name="w8p", align_bytes=64, offset=36864)
@@ -187,8 +184,8 @@ def tile_list_spectrum_probe_contrast_kernel(
                 start=start, stop=stop,
             )
 
-        def open_diff(c, t):
-            diff[c, t] = psb.tile([P, CH], F32, name="acc_v")
+        def open_diff(c, t, bank):
+            diff[c, t] = psum.tile([P, CH], F32, name=f"bank{bank}")
             w1_pass(c, t, 0, True, False)
 
         def w8_passes(c, t):
@@ -206,20 +203,23 @@ def tile_list_spectrum_probe_contrast_kernel(
             nc.vector.scalar_tensor_tensor(hs[c][:, t, :], diff[c, t][:], -1.0, recip[c, t][:], ALU.mult, ALU.mult)
             nc.sync.dma_start(out1v[:, t, c * CH:(c + 1) * CH], hs[c][:, t, :])
 
-        obf = keep.tile([P, (PASSES + 1) * N * PACK], BF16, name="obf", align_bytes=64)
+        obf = {}
         oq = keep.tile([P, (PASSES + 1) * N], U32, name="oq", align_bytes=64)
         osc = keep.tile([P, (PASSES + 1) * N], U8, name="osc", align_bytes=64)
 
-        def cast_o(src, slot, on_scalar=False):
-            dst = obf[:, slot * N * PACK:(slot + 1) * N * PACK].rearrange("p (c i j) -> p c j i", i=4, j=PACK)
+        def cast_o(src, slot, behind, on_scalar=False):
+            obf[slot] = keep.tile([P, N * PACK], BF16, name=f"obf{slot}", tag=behind, align_bytes=64)
+            dst = obf[slot][:].rearrange("p (c i j) -> p c j i", i=4, j=PACK)
             view = src[:].rearrange("p (j c i) -> p c j i", i=4, j=PACK)
             if on_scalar:
                 nc.scalar.activation(out=dst, in_=view, func=ACT.Copy)
             else:
                 nc.vector.tensor_copy(dst, view)
 
-        def quant_o(lo, hi):
-            nc.vector.quantize_mx(out=oq[:, lo:hi].bitcast(FP8X4), scales=osc[:, lo:hi], in_=obf[:, PACK * lo:PACK * hi])
+        def quant_o(slot):
+            for lo, hi in ((0, 256), (256, N)):
+                cols = slice(slot * N + lo, slot * N + hi)
+                nc.vector.quantize_mx(out=oq[:, cols].bitcast(FP8X4), scales=osc[:, cols], in_=obf[slot][:, PACK * lo:PACK * hi])
 
         hq = keep.tile([P, S], U32, name="hq", align_bytes=64)
         hsc = keep.tile([P, S], U8, name="hsc", align_bytes=64)
@@ -240,8 +240,8 @@ def tile_list_spectrum_probe_contrast_kernel(
 
         raws = {}
 
-        def raw_product(c, j):
-            raws[c, j] = psb.tile([P, CH], F32, name="acc_v")
+        def raw_product(c, j, bank):
+            raws[c, j] = psum.tile([P, CH], F32, name=f"bank{bank}")
             for a in range(PASSES):
                 col = a * N + j * P
                 nc.tensor.matmul_mx(
@@ -251,9 +251,9 @@ def tile_list_spectrum_probe_contrast_kernel(
                     start=(a == 0), stop=(a == PASSES - 1),
                 )
 
-        def readout(c, j):
+        def readout(c, j, bank):
             cols = slice(c * CH, (c + 1) * CH)
-            gate = psa.tile([P, CH], F32, name="acc_s")
+            gate = psum.tile([P, CH], F32, name=f"bank{bank}")
             col = PASSES * N + j * P
             nc.tensor.matmul_mx(
                 out=gate[:],
@@ -269,62 +269,67 @@ def tile_list_spectrum_probe_contrast_kernel(
 
         gather(0, 0)
         gather(0, 1)
-        load_rows(wrraw[1], wr, 1)
+        load_rows(wrraw[0], wr, 0)
         cast_w1(0, True)
-        load_rows(wgraw, wg, 0)
+        load_rows(wrraw[1], wr, 1)
         deal_w4_scales()
         gather(1, 0)
-        both(0, 0)
-        both(0, 1)
+        both(0, 0, 0)
+        both(0, 1, 1)
         invert(0, 0)
-        both(0, 2)
+        both(0, 2, 2)
         gather(1, 1)
+        load_rows(wgraw, wg, 0)
         quant_w1(0)
         deal_w8()
-        both(0, 3)
+        both(0, 3, 0)
         invert(0, 1)
+        invert(0, 2)
+        invert(0, 3)
         cast_w1(1, False)
         for t in range(PACK):
-            open_diff(0, t)
-        both(1, 0)
-        invert(0, 2)
+            open_diff(0, t, 3 + t)
         quant_w1(1)
         for t in range(PACK):
             w8_passes(0, t)
-        both(1, 1)
-        invert(0, 3)
+        cast_o(wrraw[0], 0, "w1bf1")
         close_diff(0, 0)
         close_diff(0, 1)
-        cast_o(wrraw[0], 0)
-        both(1, 2)
+        both(1, 0, 7)
         invert(1, 0)
         close_diff(0, 2)
+        quant_o(0)
         close_diff(0, 3)
-        cast_o(wrraw[1], 1)
-        both(1, 3)
-        invert(1, 1)
-        invert(1, 2)
-        invert(1, 3)
+        cast_o(wrraw[1], 1, "recip0_1")
         cast_h(0)
-        quant_o(0, 512)
-        quant_o(512, 768)
-        cast_o(wgraw, 2)
-        quant_h(0)
-        for t in range(PACK):
-            open_diff(1, t)
+        quant_o(1)
+
+        def whole_diff(t, bank):
+            open_diff(1, t, bank)
             w8_passes(1, t)
             close_diff(1, t)
-            if t == 0:
-                quant_o(768, 1024)
-                quant_o(1024, 1152)
+
+        whole_diff(0, 3)
+        both(1, 1, 4)
+        invert(1, 1)
+        quant_h(0)
+        cast_o(wgraw, 2, "recip0_3")
+        whole_diff(1, 5)
+        both(1, 2, 7)
+        invert(1, 2)
+        quant_o(2)
+        whole_diff(2, 6)
+        both(1, 3, 4)
+        invert(1, 3)
+        whole_diff(3, 3)
         cast_h(1)
         for j in range(NT):
-            raw_product(0, j)
+            raw_product(0, j, j)
         quant_h(1)
         for j in range(NT):
-            readout(0, j)
+            readout(0, j, (7, 4, 5)[j])
         for q in range(4):
             nc.sync.dma_start(out_3[0, 4 * q:4 * q + 4, :].bitcast(I32), hsc[32 * q:32 * q + 4, :].bitcast(I32))
         for j in range(NT):
-            raw_product(1, j)
-            readout(1, j)
+            raw_product(1, j, (6, 3, 0)[j])
+            readout(1, j, (7, 4, 5)[j])

@@ -23,6 +23,7 @@ PASSES = K // KP
 CH = 512
 CHUNKS = S // CH
 NT = N // P
+HALF = CH // 2
 
 
 def tile_list_spectrum_probe_contrast_kernel(
@@ -44,29 +45,27 @@ def tile_list_spectrum_probe_contrast_kernel(
         warm2 = keep.tile([P, 1], F32, name="warm2")
         w8sc = keep.tile([P, H], U8, name="w8sc", align_bytes=64)
         vs = keep.tile([P, S], U8, name="vs", align_bytes=64)
-        for q in range(4):
-            nc.vector.memset(tsc[32 * q:32 * q + 24, :].bitcast(I32), 0)
+        nc.vector.memset(tsc[:].bitcast(I32), 0)
         nc.gpsimd.memset(wsc[:].bitcast(I32), 0)
         nc.gpsimd.memset(warm[:], 1.0)
         nc.gpsimd.memset(w8sc[:].bitcast(I32), 0)
-        nc.vector.memset(vs[:].bitcast(I32), 0)
-        nc.vector.memset(vs1[:].bitcast(I32), 0)
+        nc.gpsimd.memset(vs1[:].bitcast(I32), 0)
         nc.scalar.activation(out=warm2[:], in_=warm[:], func=ACT.Abs_reciprocal_sqrt)
 
         nc.sync.dma_start(offsets[:], offs)
-        tabw = [turns.tile([P, T], I32, name=f"tabw{a}", align_bytes=64, offset=(20480, 36864)[a]) for a in range(PASSES)]
-        w1raw = [turns.tile([P, PACK * H], F32, name=f"w1raw{a}", align_bytes=64, offset=(28672, 6080)[a]) for a in range(PASSES)]
-        wrraw = [turns.tile([P, PACK * N], F32, name=f"wrraw{a}", align_bytes=64, offset=(14400, 28672)[a]) for a in range(PASSES)]
-        wgraw = turns.tile([P, PACK * N], F32, name="wgraw", align_bytes=64, offset=43520)
-        w4raw = turns.tile([P, PASSES * 2 * H], U8, name="w4raw", align_bytes=64, offset=4096)
-        w8raw = turns.tile([P, PASSES * H], I32, name="w8raw", align_bytes=64, offset=64)
+        tabw = [turns.tile([P, T], I32, name=f"tabw{a}", align_bytes=64, offset=(8128, 30528)[a]) for a in range(PASSES)]
+        w1raw = [turns.tile([P, PACK * H], F32, name=f"w1raw{a}", align_bytes=64, offset=(0, 16256)[a]) for a in range(PASSES)]
+        wrraw = [turns.tile([P, PACK * N], F32, name=f"wrraw{a}", align_bytes=64, offset=(8192, 24448)[a]) for a in range(PASSES)]
+        wgraw = turns.tile([P, PACK * N], F32, name="wgraw", align_bytes=64, offset=0)
+        w4raw = keep.tile([P, PASSES * 2 * H], U8, name="w4raw", align_bytes=64)
+        w8raw = keep.tile([P, PASSES * H], I32, name="w8raw", align_bytes=64)
         lev = keep.tile([P, PACK], F32, name="lev")
 
         def load_tab(a):
             nc.sync.dma_start(tabw[a][:], tab_words[a].rearrange("p t i -> p (t i)").bitcast(I32))
 
-        def load_rows(dst, src, a):
-            nc.sync.dma_start(dst[:], src[a * KP:(a + 1) * KP, :].rearrange("(p j) c -> p (j c)", j=PACK))
+        def load_rows(dst, src, a, queue=nc.sync):
+            queue.dma_start(dst[:], src[a * KP:(a + 1) * KP, :].rearrange("(p j) c -> p (j c)", j=PACK))
 
         def load_wscales(eng, src, row0):
             for q in range(4):
@@ -75,37 +74,32 @@ def tile_list_spectrum_probe_contrast_kernel(
                     src[:, 4 * q:4 * q + 4, :].bitcast(I32).rearrange("a r c -> r a c"),
                 )
 
-        for q in range(4):
-            nc.sync.dma_start(tsc[32 * q + 24:32 * q + 32, :].bitcast(I32), tab_scales[:, 4 * q:4 * q + 4, :].bitcast(I32))
         nc.sync.dma_start(
             w4raw[:].bitcast(I32).rearrange("p (a c) -> p a c", a=PASSES),
             w4_words.bitcast(I32).rearrange("a p c -> p a c"),
         )
+        for q in range(4):
+            nc.sync.dma_start(tsc[32 * q:32 * q + 8, :].bitcast(I32), tab_scales[:, 4 * q:4 * q + 4, :].bitcast(I32))
         nc.gpsimd.dma_start(lev[:], level.rearrange("(p t) -> p t", t=PACK))
         for q in range(4):
             nc.gpsimd.dma_start(w8sc[32 * q:32 * q + 8, :].bitcast(I32), w8_scales[:, 4 * q:4 * q + 4, :].bitcast(I32))
         load_tab(0)
-        load_rows(w1raw[0], w1, 0)
         load_wscales(nc.sync, w4_scales, 0)
         load_tab(1)
-
-        vsg = keep.tile([P, S], U8, name="vsg", align_bytes=64)
-        nc.vector.tensor_copy(vsg[:], tsc[:].indirect(offsets[:]))
-        nc.scalar.dma_start(vs[0:104, :].bitcast(I32), vsg[24:128, :].bitcast(I32))
-        nc.scalar.dma_start(vs1[0:100, :].bitcast(I32), vsg[28:128, :].bitcast(I32))
-
-        w4p = keep.tile([P, PASSES * 2 * H], U8, name="w4p", align_bytes=64)
-        nc.vector.tensor_copy(
-            w4p[:].rearrange("p (a t m b) -> p a t m b", a=PASSES, t=PACK, b=2),
-            w4raw[:].rearrange("p (a m t b) -> p a t m b", a=PASSES, t=PACK, b=2),
-        )
         nc.sync.dma_start(
             w8raw[:].rearrange("p (a c) -> p a c", a=PASSES),
             w8_words.rearrange("a p c i -> p a (c i)").bitcast(I32),
         )
-        load_rows(w1raw[1], w1, 1)
-        wscp = turns.tile([P, PASSES * H], U8, name="wscp", align_bytes=64, offset=26624)
-        w8scp = turns.tile([P, H], U8, name="w8scp", align_bytes=64, offset=40960)
+
+        w4p = keep.tile([P, PASSES * 2 * H], U8, name="w4p", align_bytes=64)
+        nc.vector.tensor_copy(
+            w4p[:].bitcast(U16).rearrange("p (a t m) -> p a t m", a=PASSES, t=PACK),
+            w4raw[:].bitcast(U16).rearrange("p (a m t) -> p a t m", a=PASSES, t=PACK),
+        )
+        nc.vector.tensor_copy(vs[:], tsc[:].indirect(offsets[:]))
+        nc.scalar.dma_start(vs1[0:112, :].bitcast(I32), vs[4:116, :].bitcast(I32))
+        wscp = keep.tile([P, PASSES * H], U8, name="wscp", align_bytes=64)
+        w8scp = turns.tile([P, H], U8, name="w8scp", align_bytes=64, offset=34688)
 
         def deal_w4_scales():
             nc.vector.tensor_copy(
@@ -129,8 +123,11 @@ def tile_list_spectrum_probe_contrast_kernel(
             cols = slice(c * (CH // 16), (c + 1) * (CH // 16))
             nc.vector.tensor_copy(vw[a][c][:], tabw[a][:].bitcast(U32).indirect(offsets[:, cols]))
 
-        w1bf = [keep.tile([P, PACK * H], BF16, name=f"w1bf{a}", tag=f"w1bf{a}", align_bytes=64) for a in range(PASSES)]
-        w1q = [turns.tile([P, H], U32, name=f"w1q{a}", align_bytes=64, offset=(41472, 49664)[a]) for a in range(PASSES)]
+        w1bf = [
+            turns.tile([P, PACK * H], BF16, name="w1bf0", align_bytes=64, offset=35200),
+            keep.tile([P, PACK * H], BF16, name="w1bf1", tag="w1bf1", align_bytes=64),
+        ]
+        w1q = [keep.tile([P, H], U32, name=f"w1q{a}", align_bytes=64) for a in range(PASSES)]
         w1s = [keep.tile([P, H], U8, name=f"w1s{a}", align_bytes=64) for a in range(PASSES)]
 
         def cast_w1(a, on_scalar):
@@ -164,13 +161,13 @@ def tile_list_spectrum_probe_contrast_kernel(
             mags[c, t] = keep.tile([P, CH], F32, name=f"mag{c}_{t}")
             nc.scalar.activation(out=mags[c, t][:], in_=acc[:], func=ACT.Abs)
 
-        def invert(c, t):
+        def invert(c, t, lo=0, hi=CH):
             root = ring.tile([P, CH], F32, name="root")
-            nc.scalar.activation(out=root[:], in_=mags[c, t][:], func=ACT.Abs_reciprocal_sqrt, bias=lev[:, t:t + 1])
-            recip[c, t] = keep.tile([P, CH], F32, name=f"recip{c}_{t}", tag=f"recip{c}_{t}", align_bytes=64)
-            nc.scalar.activation(out=recip[c, t][:], in_=root[:], func=ACT.Square)
+            nc.scalar.activation(out=root[:, lo:hi], in_=mags[c, t][:, lo:hi], func=ACT.Abs_reciprocal_sqrt, bias=lev[:, t:t + 1])
+            recip[c, t, lo] = keep.tile([P, hi - lo], F32, name=f"recip{c}_{t}_{lo}", tag=f"recip{c}_{t}_{lo}", align_bytes=64)
+            nc.scalar.activation(out=recip[c, t, lo][:], in_=root[:, lo:hi], func=ACT.Square)
 
-        w8p = turns.tile([P, PASSES * H], I32, name="w8p", align_bytes=64, offset=36864)
+        w8p = turns.tile([P, PASSES * H], I32, name="w8p", align_bytes=64, offset=30592)
         hs = [keep.tile([P, PACK, CH], F32, name=f"h{c}", align_bytes=64) for c in range(CHUNKS)]
         out1v = out_1.rearrange("(p t) s -> p t s", t=PACK)
 
@@ -184,42 +181,37 @@ def tile_list_spectrum_probe_contrast_kernel(
                 start=start, stop=stop,
             )
 
-        def open_diff(c, t, bank):
+        def open_diff(c, t, bank, a):
             diff[c, t] = psum.tile([P, CH], F32, name=f"bank{bank}")
-            w1_pass(c, t, 0, True, False)
+            w1_pass(c, t, a, True, False)
 
-        def w8_passes(c, t):
+        def w8_passes(c, t, start=False):
             for a in range(PASSES):
                 col = a * H + t * P
                 nc.tensor.matmul_mx(
                     out=diff[c, t][:],
                     lhsT=w8p[:, col:col + P].bitcast(FP8X4), lhsT_scale=w8scp[4 * a:, t * P:(t + 1) * P],
                     rhs=vw[a][c][:].bitcast(FP8X4), rhs_scale=vscale(a, c),
-                    start=False, stop=False,
+                    start=(start and a == 0), stop=False,
                 )
 
-        def close_diff(c, t):
-            w1_pass(c, t, 1, False, True)
-            nc.vector.scalar_tensor_tensor(hs[c][:, t, :], diff[c, t][:], -1.0, recip[c, t][:], ALU.mult, ALU.mult)
-            nc.sync.dma_start(out1v[:, t, c * CH:(c + 1) * CH], hs[c][:, t, :])
+        def contrast(c, t, lo=0, hi=CH):
+            nc.vector.scalar_tensor_tensor(hs[c][:, t, lo:hi], diff[c, t][:, lo:hi], -1.0, recip[c, t, lo][:], ALU.mult, ALU.mult)
+            if hi == CH:
+                nc.sync.dma_start(out1v[:, t, c * CH:(c + 1) * CH], hs[c][:, t, :])
 
-        obf = {}
         oq = keep.tile([P, (PASSES + 1) * N], U32, name="oq", align_bytes=64)
         osc = keep.tile([P, (PASSES + 1) * N], U8, name="osc", align_bytes=64)
 
-        def cast_o(src, slot, behind, on_scalar=False):
-            obf[slot] = keep.tile([P, N * PACK], BF16, name=f"obf{slot}", tag=behind, align_bytes=64)
-            dst = obf[slot][:].rearrange("p (c i j) -> p c j i", i=4, j=PACK)
-            view = src[:].rearrange("p (j c i) -> p c j i", i=4, j=PACK)
-            if on_scalar:
-                nc.scalar.activation(out=dst, in_=view, func=ACT.Copy)
-            else:
-                nc.vector.tensor_copy(dst, view)
+        def cast_rows(dst, src):
+            nc.vector.tensor_copy(
+                dst.rearrange("p (c i j) -> p c j i", i=4, j=PACK),
+                src[:].rearrange("p (j c i) -> p c j i", i=4, j=PACK),
+            )
 
-        def quant_o(slot):
-            for lo, hi in ((0, 256), (256, N)):
-                cols = slice(slot * N + lo, slot * N + hi)
-                nc.vector.quantize_mx(out=oq[:, cols].bitcast(FP8X4), scales=osc[:, cols], in_=obf[slot][:, PACK * lo:PACK * hi])
+        def quant_o(src, col0, lo, hi):
+            cols = slice(col0 + lo, col0 + hi)
+            nc.vector.quantize_mx(out=oq[:, cols].bitcast(FP8X4), scales=osc[:, cols], in_=src[:, PACK * lo:PACK * hi])
 
         hq = keep.tile([P, S], U32, name="hq", align_bytes=64)
         hsc = keep.tile([P, S], U8, name="hsc", align_bytes=64)
@@ -227,18 +219,21 @@ def tile_list_spectrum_probe_contrast_kernel(
 
         hbf = [keep.tile([P, CH * PACK], BF16, name=f"hbf{c}", align_bytes=64) for c in range(CHUNKS)]
 
-        def cast_h(c):
+        def cast_h(c, lo=0, hi=CH):
             nc.vector.tensor_copy(
-                hbf[c][:].rearrange("p (c i t) -> p c t i", i=4, t=PACK),
-                hs[c][:].rearrange("p t (c i) -> p c t i", i=4),
+                hbf[c][:, PACK * lo:PACK * hi].rearrange("p (c i t) -> p c t i", i=4, t=PACK),
+                hs[c][:, :, lo:hi].rearrange("p t (c i) -> p c t i", i=4),
             )
 
-        def quant_h(c):
-            cols = slice(c * CH, (c + 1) * CH)
-            nc.vector.quantize_mx(out=hq[:, cols].bitcast(FP8X4), scales=hsc[:, cols], in_=hbf[c][:])
-            nc.sync.dma_start(out2v[:, cols], hq[:, cols].bitcast(I32))
+        def quant_h(c, lo=0, hi=CH):
+            cols = slice(c * CH + lo, c * CH + hi)
+            nc.vector.quantize_mx(out=hq[:, cols].bitcast(FP8X4), scales=hsc[:, cols], in_=hbf[c][:, PACK * lo:PACK * hi])
+            if hi == CH:
+                whole = slice(c * CH, (c + 1) * CH)
+                nc.sync.dma_start(out2v[:, whole], hq[:, whole].bitcast(I32))
 
         raws = {}
+        sigs = {}
 
         def raw_product(c, j, bank):
             raws[c, j] = psum.tile([P, CH], F32, name=f"bank{bank}")
@@ -261,75 +256,93 @@ def tile_list_spectrum_probe_contrast_kernel(
                 rhs=hq[:, cols].bitcast(FP8X4), rhs_scale=hsc[:, cols],
                 start=True, stop=True,
             )
-            sig = ring.tile([P, CH], F32, name="sig")
-            nc.scalar.activation(out=sig[:], in_=gate[:], func=ACT.Sigmoid)
+            sigs[c, j] = keep.tile([P, CH], F32, name=f"sig{c}_{j}")
+            nc.scalar.activation(out=sigs[c, j][:], in_=gate[:], func=ACT.Sigmoid)
+
+        def finish(c, j):
+            cols = slice(c * CH, (c + 1) * CH)
             y = ring.tile([P, CH], F32, name="y")
-            nc.vector.tensor_tensor(y[:], raws[c, j][:], sig[:], ALU.mult)
+            nc.vector.tensor_tensor(y[:], raws[c, j][:], sigs[c, j][:], ALU.mult)
             nc.sync.dma_start(out_0[j * P:(j + 1) * P, cols], y[:])
 
         gather(0, 0)
         gather(0, 1)
+        load_rows(w1raw[0], w1, 0)
+        load_rows(w1raw[1], w1, 1)
         load_rows(wrraw[0], wr, 0)
-        cast_w1(0, True)
-        load_rows(wrraw[1], wr, 1)
         deal_w4_scales()
         gather(1, 0)
         both(0, 0, 0)
         both(0, 1, 1)
         invert(0, 0)
         both(0, 2, 2)
-        gather(1, 1)
-        load_rows(wgraw, wg, 0)
-        quant_w1(0)
-        deal_w8()
-        both(0, 3, 0)
+        both(0, 3, 7)
         invert(0, 1)
+        gather(1, 1)
+        load_rows(wrraw[1], wr, 1)
+        deal_w8()
+        cast_w1(0, False)
+        load_rows(wgraw, wg, 0)
+        both(1, 0, 0)
         invert(0, 2)
+        both(1, 1, 1)
         invert(0, 3)
+        quant_w1(0)
         cast_w1(1, False)
         for t in range(PACK):
-            open_diff(0, t, 3 + t)
+            diff[0, t] = psum.tile([P, CH], F32, name=f"bank{3 + t}")
+            w8_passes(0, t, True)
         quant_w1(1)
+        both(1, 2, 2)
+        invert(1, 0, 0, HALF)
+        both(1, 3, 7)
+        for t in range(1, PACK):
+            invert(1, t, 0, HALF)
         for t in range(PACK):
-            w8_passes(0, t)
-        cast_o(wrraw[0], 0, "w1bf1")
-        close_diff(0, 0)
-        close_diff(0, 1)
-        both(1, 0, 7)
-        invert(1, 0)
-        close_diff(0, 2)
-        quant_o(0)
-        close_diff(0, 3)
-        cast_o(wrraw[1], 1, "recip0_1")
+            w1_pass(0, t, 0, False, False)
+        wrbf = keep.tile([P, PASSES * N * PACK], BF16, name="wrbf", tag="w1bf1", align_bytes=64)
+        for a in range(PASSES):
+            cast_rows(wrbf[:, a * N * PACK:(a + 1) * N * PACK], wrraw[a])
+        for t in range(PACK):
+            w1_pass(0, t, 1, False, True)
+        contrast(0, 0)
+        quant_o(wrbf, 0, 0, 512)
+        quant_o(wrbf, 0, 512, 768)
+        for t in range(1, PACK):
+            contrast(0, t)
         cast_h(0)
-        quant_o(1)
+        wgbf = keep.tile([P, N * PACK], BF16, name="wgbf", tag="recip0_3_0", align_bytes=64)
+        cast_rows(wgbf[:], wgraw)
+        quant_h(0)
+        quant_o(wgbf, 768, 0, 256)
+        quant_o(wgbf, 768, 256, 384)
 
         def whole_diff(t, bank):
-            open_diff(1, t, bank)
+            open_diff(1, t, bank, 1)
             w8_passes(1, t)
-            close_diff(1, t)
+            w1_pass(1, t, 0, False, True)
+            contrast(1, t, 0, HALF)
 
-        whole_diff(0, 3)
-        both(1, 1, 4)
-        invert(1, 1)
-        quant_h(0)
-        cast_o(wgraw, 2, "recip0_3")
-        whole_diff(1, 5)
-        both(1, 2, 7)
-        invert(1, 2)
-        quant_o(2)
-        whole_diff(2, 6)
-        both(1, 3, 4)
-        invert(1, 3)
-        whole_diff(3, 3)
-        cast_h(1)
+        for t in range(PACK):
+            whole_diff(t, (0, 1, 2, 7)[t])
+        cast_h(1, 0, HALF)
+        for t in range(PACK):
+            invert(1, t, HALF, CH)
+            contrast(1, t, HALF, CH)
+            if t == 0:
+                quant_h(1, 0, HALF)
+        cast_h(1, HALF, CH)
         for j in range(NT):
-            raw_product(0, j, j)
-        quant_h(1)
+            raw_product(0, j, 3 + j)
         for j in range(NT):
-            readout(0, j, (7, 4, 5)[j])
+            readout(0, j, (6, 0, 1)[j])
+        quant_h(1, HALF, CH)
         for q in range(4):
             nc.sync.dma_start(out_3[0, 4 * q:4 * q + 4, :].bitcast(I32), hsc[32 * q:32 * q + 4, :].bitcast(I32))
         for j in range(NT):
-            raw_product(1, j, (6, 3, 0)[j])
-            readout(1, j, (7, 4, 5)[j])
+            finish(0, j)
+        for j in range(NT):
+            raw_product(1, j, (2, 7, 3)[j])
+            readout(1, j, (6, 0, 1)[j])
+        for j in range(NT):
+            finish(1, j)

@@ -44,21 +44,24 @@ def tile_list_spectrum_probe_contrast_kernel(
         warm = keep.tile([P, 1], F32, name="warm")
         warm2 = keep.tile([P, 1], F32, name="warm2")
         w8sc = keep.tile([P, H], U8, name="w8sc", align_bytes=64)
-        vs = keep.tile([P, S], U8, name="vs", align_bytes=64)
+        vs = [
+            keep.tile([P, CH], U8, name="gsc0", align_bytes=64),
+            keep.tile([P, CH], U8, name="gsc1", align_bytes=64),
+        ]
         nc.vector.memset(tsc[:].bitcast(I32), 0)
-        nc.gpsimd.memset(wsc[:].bitcast(I32), 0)
-        nc.gpsimd.memset(warm[:], 1.0)
         nc.gpsimd.memset(w8sc[:].bitcast(I32), 0)
-        nc.gpsimd.memset(vs1[:].bitcast(I32), 0)
+        nc.vector.memset(warm[:], 1.0)
+        nc.vector.memset(wsc[:].bitcast(I32), 0)
+        nc.vector.memset(vs1[:].bitcast(I32), 0)
         nc.scalar.activation(out=warm2[:], in_=warm[:], func=ACT.Abs_reciprocal_sqrt)
 
         nc.sync.dma_start(offsets[:], offs)
-        tabw = [turns.tile([P, T], I32, name=f"tabw{a}", align_bytes=64, offset=(8128, 30528)[a]) for a in range(PASSES)]
-        w1raw = [turns.tile([P, PACK * H], F32, name=f"w1raw{a}", align_bytes=64, offset=(0, 16256)[a]) for a in range(PASSES)]
-        wrraw = [turns.tile([P, PACK * N], F32, name=f"wrraw{a}", align_bytes=64, offset=(8192, 24448)[a]) for a in range(PASSES)]
-        wgraw = turns.tile([P, PACK * N], F32, name="wgraw", align_bytes=64, offset=0)
+        tabw = [turns.tile([P, T], I32, name=f"tabw{a}", align_bytes=64, offset=(8192, 16384)[a]) for a in range(PASSES)]
+        w1raw = [turns.tile([P, PACK * H], F32, name=f"w1raw{a}", align_bytes=64, offset=(24576, 32768)[a]) for a in range(PASSES)]
+        wrraw = [keep.tile([P, PACK * N], F32, name=f"wrraw{a}", align_bytes=64) for a in range(PASSES)]
+        wgraw = keep.tile([P, PACK * N], F32, name="wgraw", align_bytes=64)
         w4raw = keep.tile([P, PASSES * 2 * H], U8, name="w4raw", align_bytes=64)
-        w8raw = keep.tile([P, PASSES * H], I32, name="w8raw", align_bytes=64)
+        w8raw = turns.tile([P, PASSES * H], I32, name="w8raw", align_bytes=64, offset=1984)
         lev = keep.tile([P, PACK], F32, name="lev")
 
         def load_tab(a):
@@ -80,26 +83,36 @@ def tile_list_spectrum_probe_contrast_kernel(
         )
         for q in range(4):
             nc.sync.dma_start(tsc[32 * q:32 * q + 8, :].bitcast(I32), tab_scales[:, 4 * q:4 * q + 4, :].bitcast(I32))
-        nc.gpsimd.dma_start(lev[:], level.rearrange("(p t) -> p t", t=PACK))
         for q in range(4):
-            nc.gpsimd.dma_start(w8sc[32 * q:32 * q + 8, :].bitcast(I32), w8_scales[:, 4 * q:4 * q + 4, :].bitcast(I32))
+            queue = nc.scalar if q < 2 else nc.gpsimd
+            queue.dma_start(w8sc[32 * q:32 * q + 8, :].bitcast(I32), w8_scales[:, 4 * q:4 * q + 4, :].bitcast(I32))
+        nc.gpsimd.dma_start(lev[:], level.rearrange("(p t) -> p t", t=PACK))
         load_tab(0)
         load_wscales(nc.sync, w4_scales, 0)
         load_tab(1)
-        nc.sync.dma_start(
-            w8raw[:].rearrange("p (a c) -> p a c", a=PASSES),
-            w8_words.rearrange("a p c i -> p a (c i)").bitcast(I32),
-        )
 
         w4p = keep.tile([P, PASSES * 2 * H], U8, name="w4p", align_bytes=64)
         nc.vector.tensor_copy(
             w4p[:].bitcast(U16).rearrange("p (a t m) -> p a t m", a=PASSES, t=PACK),
             w4raw[:].bitcast(U16).rearrange("p (a m t) -> p a t m", a=PASSES, t=PACK),
         )
-        nc.vector.tensor_copy(vs[:], tsc[:].indirect(offsets[:]))
-        nc.scalar.dma_start(vs1[0:112, :].bitcast(I32), vs[4:116, :].bitcast(I32))
+        def gather_scales(c):
+            nc.vector.tensor_copy(vs[c][:], tsc[:].indirect(offsets[:, c * (CH // 16):(c + 1) * (CH // 16)]))
+            nc.scalar.dma_start(vs1[0:112, c * CH:(c + 1) * CH].bitcast(I32), vs[c][4:116, :].bitcast(I32))
+
+        gather_scales(0)
+        gather_scales(1)
+        nc.sync.dma_start(
+            w8raw[:].rearrange("p (a c) -> p a c", a=PASSES),
+            w8_words.rearrange("a p c i -> p a (c i)").bitcast(I32),
+        )
+        load_rows(w1raw[0], w1, 0)
+        load_rows(w1raw[1], w1, 1)
+        load_rows(wrraw[0], wr, 0)
+        load_rows(wrraw[1], wr, 1)
+        load_rows(wgraw, wg, 0)
         wscp = keep.tile([P, PASSES * H], U8, name="wscp", align_bytes=64)
-        w8scp = turns.tile([P, H], U8, name="w8scp", align_bytes=64, offset=34688)
+        w8scp = turns.tile([P, H], U8, name="w8scp", align_bytes=64, offset=2048)
 
         def deal_w4_scales():
             nc.vector.tensor_copy(
@@ -117,16 +130,17 @@ def tile_list_spectrum_probe_contrast_kernel(
                 w8sc[:].rearrange("p (m t) -> p t m", t=PACK),
             )
 
-        vw = [[keep.tile([P, CH], U32, name=f"vw{a}_{c}", align_bytes=64) for c in range(CHUNKS)] for a in range(PASSES)]
+        vw = [
+            [keep.tile([P, CH], U32, name=f"vw{a}_0", align_bytes=64),
+             turns.tile([P, CH], U32, name=f"vw{a}_1", align_bytes=64, offset=(0, 4032)[a])]
+            for a in range(PASSES)
+        ]
 
         def gather(a, c):
             cols = slice(c * (CH // 16), (c + 1) * (CH // 16))
             nc.vector.tensor_copy(vw[a][c][:], tabw[a][:].bitcast(U32).indirect(offsets[:, cols]))
 
-        w1bf = [
-            turns.tile([P, PACK * H], BF16, name="w1bf0", align_bytes=64, offset=35200),
-            keep.tile([P, PACK * H], BF16, name="w1bf1", tag="w1bf1", align_bytes=64),
-        ]
+        w1bf = [turns.tile([P, PACK * H], BF16, name=f"w1bf{a}", align_bytes=64, offset=(14336, 24576)[a]) for a in range(PASSES)]
         w1q = [keep.tile([P, H], U32, name=f"w1q{a}", align_bytes=64) for a in range(PASSES)]
         w1s = [keep.tile([P, H], U8, name=f"w1s{a}", align_bytes=64) for a in range(PASSES)]
 
@@ -142,32 +156,47 @@ def tile_list_spectrum_probe_contrast_kernel(
             nc.vector.quantize_mx(out=w1q[a][:].bitcast(FP8X4), scales=w1s[a][:], in_=w1bf[a][:])
 
         def vscale(a, c):
-            return vs[4 * a:, c * CH:(c + 1) * CH]
+            return vs[c][4 * a:, :]
 
         recip = {}
         mags = {}
 
-        def both(c, t, bank):
-            acc = psum.tile([P, CH], F32, name=f"bank{bank}")
-            for a in range(PASSES):
-                col = a * H + t * P
-                plane = vs if a == 0 else vs1
-                nc.tensor.matmul_mx(
-                    out=acc[:],
-                    lhsT=w4p[:, 2 * col:2 * (col + P)].bitcast(FP4X4), lhsT_scale=wscp[:, col:col + P],
-                    rhs=vw[a][c][:].bitcast(FP8X4), rhs_scale=plane[:, c * CH:(c + 1) * CH],
-                    start=(a == 0), stop=(a == PASSES - 1),
-                )
-            mags[c, t] = keep.tile([P, CH], F32, name=f"mag{c}_{t}")
-            nc.scalar.activation(out=mags[c, t][:], in_=acc[:], func=ACT.Abs)
+        sums = {}
 
-        def invert(c, t, lo=0, hi=CH):
-            root = ring.tile([P, CH], F32, name="root")
-            nc.scalar.activation(out=root[:, lo:hi], in_=mags[c, t][:, lo:hi], func=ACT.Abs_reciprocal_sqrt, bias=lev[:, t:t + 1])
-            recip[c, t, lo] = keep.tile([P, hi - lo], F32, name=f"recip{c}_{t}_{lo}", tag=f"recip{c}_{t}_{lo}", align_bytes=64)
-            nc.scalar.activation(out=recip[c, t, lo][:], in_=root[:, lo:hi], func=ACT.Square)
+        def both_pass(c, t, a, first=0):
+            if a == first:
+                sums[c, t] = psum.tile([P, CH], F32, name=f"bank{t}")
+            col = a * H + t * P
+            plane = vs[c][:] if a == 0 else vs1[:, c * CH:(c + 1) * CH]
+            nc.tensor.matmul_mx(
+                out=sums[c, t][:],
+                lhsT=w4p[:, 2 * col:2 * (col + P)].bitcast(FP4X4), lhsT_scale=wscp[:, col:col + P],
+                rhs=vw[a][c][:].bitcast(FP8X4), rhs_scale=plane,
+                start=(a == first), stop=(a != first),
+            )
 
-        w8p = turns.tile([P, PASSES * H], I32, name="w8p", align_bytes=64, offset=30592)
+        def magnitude(c, t):
+            mags[c, t] = keep.tile([P, CH], F32, name=f"mag{c}_{t}", tag=f"mag{c}_{t}", align_bytes=64)
+            nc.scalar.activation(out=mags[c, t][:], in_=sums[c, t][:], func=ACT.Abs)
+
+        roots = {}
+
+        def inverse_root(c, t):
+            roots[c, t] = ring.tile([P, CH], F32, name="root")
+            nc.scalar.activation(out=roots[c, t][:], in_=mags[c, t][:], func=ACT.Abs_reciprocal_sqrt, bias=lev[:, t:t + 1])
+
+        def square(c, t):
+            recip[c, t, 0] = keep.tile([P, CH], F32, name=f"recip{c}_{t}", align_bytes=64)
+            nc.scalar.activation(out=recip[c, t, 0][:], in_=roots[c, t][:], func=ACT.Square)
+
+        def invert_all(c):
+            for t in range(PACK + 1):
+                if t < PACK:
+                    inverse_root(c, t)
+                if t > 0:
+                    square(c, t - 1)
+
+        w8p = keep.tile([P, PASSES * H], I32, name="w8p", align_bytes=64)
         hs = [keep.tile([P, PACK, CH], F32, name=f"h{c}", align_bytes=64) for c in range(CHUNKS)]
         out1v = out_1.rearrange("(p t) s -> p t s", t=PACK)
 
@@ -203,8 +232,8 @@ def tile_list_spectrum_probe_contrast_kernel(
         oq = keep.tile([P, (PASSES + 1) * N], U32, name="oq", align_bytes=64)
         osc = keep.tile([P, (PASSES + 1) * N], U8, name="osc", align_bytes=64)
 
-        def cast_rows(dst, src):
-            nc.vector.tensor_copy(
+        def cast_rows(dst, src, copy=nc.vector.tensor_copy):
+            copy(
                 dst.rearrange("p (c i j) -> p c j i", i=4, j=PACK),
                 src[:].rearrange("p (j c i) -> p c j i", i=4, j=PACK),
             )
@@ -261,88 +290,70 @@ def tile_list_spectrum_probe_contrast_kernel(
 
         def finish(c, j):
             cols = slice(c * CH, (c + 1) * CH)
-            y = ring.tile([P, CH], F32, name="y")
+            y = keep.tile([P, CH], F32, name=f"y{c}_{j}")
             nc.vector.tensor_tensor(y[:], raws[c, j][:], sigs[c, j][:], ALU.mult)
             nc.sync.dma_start(out_0[j * P:(j + 1) * P, cols], y[:])
 
         gather(0, 0)
-        gather(0, 1)
-        load_rows(w1raw[0], w1, 0)
-        load_rows(w1raw[1], w1, 1)
-        load_rows(wrraw[0], wr, 0)
         deal_w4_scales()
         gather(1, 0)
-        both(0, 0, 0)
-        both(0, 1, 1)
-        invert(0, 0)
-        both(0, 2, 2)
-        both(0, 3, 7)
-        invert(0, 1)
-        gather(1, 1)
-        load_rows(wrraw[1], wr, 1)
+        for a in range(PASSES):
+            for t in range(2):
+                both_pass(0, t, a)
+        for t in range(2, PACK):
+            both_pass(0, t, 1, 1)
+            both_pass(0, t, 0, 1)
+        for t in range(PACK):
+            magnitude(0, t)
         deal_w8()
-        cast_w1(0, False)
-        load_rows(wgraw, wg, 0)
-        both(1, 0, 0)
-        invert(0, 2)
-        both(1, 1, 1)
-        invert(0, 3)
-        quant_w1(0)
-        cast_w1(1, False)
+        gather(0, 1)
+        gather(1, 1)
         for t in range(PACK):
-            diff[0, t] = psum.tile([P, CH], F32, name=f"bank{3 + t}")
+            diff[0, t] = psum.tile([P, CH], F32, name=f"bank{4 + t}")
             w8_passes(0, t, True)
-        quant_w1(1)
-        both(1, 2, 2)
-        invert(1, 0, 0, HALF)
-        both(1, 3, 7)
-        for t in range(1, PACK):
-            invert(1, t, 0, HALF)
         for t in range(PACK):
-            w1_pass(0, t, 0, False, False)
-        wrbf = keep.tile([P, PASSES * N * PACK], BF16, name="wrbf", tag="w1bf1", align_bytes=64)
+            for a in range(PASSES):
+                both_pass(1, t, a)
+        invert_all(0)
+        for t in range(PACK):
+            magnitude(1, t)
+        for a in range(PASSES):
+            cast_w1(a, False)
+            quant_w1(a)
+            for t in range(PACK):
+                w1_pass(0, t, a, False, a == PASSES - 1)
+        wrbf = turns.tile([P, PASSES * N * PACK], BF16, name="wrbf", align_bytes=64, offset=24576)
+        wgbf = keep.tile([P, N * PACK], BF16, name="wgbf", tag="mag1_3", align_bytes=64)
         for a in range(PASSES):
             cast_rows(wrbf[:, a * N * PACK:(a + 1) * N * PACK], wrraw[a])
-        for t in range(PACK):
-            w1_pass(0, t, 1, False, True)
-        contrast(0, 0)
+            contrast(0, 2 * a)
+            contrast(0, 2 * a + 1)
         quant_o(wrbf, 0, 0, 512)
-        quant_o(wrbf, 0, 512, 768)
-        for t in range(1, PACK):
-            contrast(0, t)
         cast_h(0)
-        wgbf = keep.tile([P, N * PACK], BF16, name="wgbf", tag="recip0_3_0", align_bytes=64)
-        cast_rows(wgbf[:], wgraw)
+        quant_o(wrbf, 0, 512, 768)
         quant_h(0)
-        quant_o(wgbf, 768, 0, 256)
-        quant_o(wgbf, 768, 256, 384)
-
-        def whole_diff(t, bank):
-            open_diff(1, t, bank, 1)
+        invert_all(1)
+        cast_rows(wgbf[:], wgraw, nc.scalar.copy)
+        for t in range(PACK):
+            open_diff(1, t, t, 1)
             w8_passes(1, t)
             w1_pass(1, t, 0, False, True)
-            contrast(1, t, 0, HALF)
-
-        for t in range(PACK):
-            whole_diff(t, (0, 1, 2, 7)[t])
-        cast_h(1, 0, HALF)
-        for t in range(PACK):
-            invert(1, t, HALF, CH)
-            contrast(1, t, HALF, CH)
-            if t == 0:
-                quant_h(1, 0, HALF)
-        cast_h(1, HALF, CH)
+            contrast(1, t)
         for j in range(NT):
-            raw_product(0, j, 3 + j)
+            raw_product(0, j, 4 + j)
+        quant_o(wgbf, 768, 0, 256)
+        quant_o(wgbf, 768, 256, 384)
+        cast_h(1)
         for j in range(NT):
-            readout(0, j, (6, 0, 1)[j])
-        quant_h(1, HALF, CH)
+            readout(0, j, (7, 0, 1)[j])
+        quant_h(1)
         for q in range(4):
             nc.sync.dma_start(out_3[0, 4 * q:4 * q + 4, :].bitcast(I32), hsc[32 * q:32 * q + 4, :].bitcast(I32))
         for j in range(NT):
             finish(0, j)
         for j in range(NT):
-            raw_product(1, j, (2, 7, 3)[j])
-            readout(1, j, (6, 0, 1)[j])
+            raw_product(1, j, (2, 3, 7)[j])
+        for j in range(NT):
+            readout(1, j, (0, 1, 4)[j])
         for j in range(NT):
             finish(1, j)

@@ -38,8 +38,9 @@ def tile_list_spectrum_probe_contrast_kernel(
         psum = ctx.enter_context(tc.psum_pool(name="psum", bufs=1))
 
         offsets = keep.tile([P, S // 16], U16, name="offsets")
-        tsc = keep.tile([P, T], U8, name="tsc", align_bytes=64)
-        wsc = keep.tile([P, PASSES * H], U8, name="wsc", align_bytes=64)
+        early = turns.tile([P, 38912], U8, name="early", align_bytes=64, offset=22528)
+        tsc = early[:, 0:T]
+        wsc = keep.tile([P, PASSES * H], U8, name="wsc", tag="wsc", align_bytes=64)
         vs1 = keep.tile([P, S], U8, name="vs1", align_bytes=64)
         warm = keep.tile([P, 1], F32, name="warm")
         warm2 = keep.tile([P, 1], F32, name="warm2")
@@ -48,7 +49,7 @@ def tile_list_spectrum_probe_contrast_kernel(
             keep.tile([P, CH], U8, name="gsc0", align_bytes=64),
             keep.tile([P, CH], U8, name="gsc1", align_bytes=64),
         ]
-        nc.vector.memset(tsc[:].bitcast(I32), 0)
+        nc.vector.memset(tsc.bitcast(I32), 0)
         nc.gpsimd.memset(w8sc[:].bitcast(I32), 0)
         nc.vector.memset(warm[:], 1.0)
         nc.vector.memset(wsc[:].bitcast(I32), 0)
@@ -56,12 +57,12 @@ def tile_list_spectrum_probe_contrast_kernel(
         nc.scalar.activation(out=warm2[:], in_=warm[:], func=ACT.Abs_reciprocal_sqrt)
 
         nc.sync.dma_start(offsets[:], offs)
-        tabw = [turns.tile([P, T], I32, name=f"tabw{a}", align_bytes=64, offset=(8192, 16384)[a]) for a in range(PASSES)]
+        tabw = [turns.tile([P, T], I32, name=f"tabw{a}", align_bytes=64, offset=(0, 8192)[a]) for a in range(PASSES)]
         w1raw = [turns.tile([P, PACK * H], F32, name=f"w1raw{a}", align_bytes=64, offset=(24576, 32768)[a]) for a in range(PASSES)]
-        wrraw = [keep.tile([P, PACK * N], F32, name=f"wrraw{a}", align_bytes=64) for a in range(PASSES)]
-        wgraw = keep.tile([P, PACK * N], F32, name="wgraw", align_bytes=64)
+        wrraw = [turns.tile([P, PACK * N], F32, name=f"wrraw{a}", align_bytes=64, offset=(40960, 47104)[a]) for a in range(PASSES)]
+        wgraw = turns.tile([P, PACK * N], F32, name="wgraw", align_bytes=64, offset=53248)
         w4raw = keep.tile([P, PASSES * 2 * H], U8, name="w4raw", align_bytes=64)
-        w8raw = turns.tile([P, PASSES * H], I32, name="w8raw", align_bytes=64, offset=1984)
+        w8raw = turns.tile([P, PASSES * H], I32, name="w8raw", align_bytes=64, offset=59392)
         lev = keep.tile([P, PACK], F32, name="lev")
 
         def load_tab(a):
@@ -82,14 +83,13 @@ def tile_list_spectrum_probe_contrast_kernel(
             w4_words.bitcast(I32).rearrange("a p c -> p a c"),
         )
         for q in range(4):
-            nc.sync.dma_start(tsc[32 * q:32 * q + 8, :].bitcast(I32), tab_scales[:, 4 * q:4 * q + 4, :].bitcast(I32))
+            nc.sync.dma_start(early[32 * q:32 * q + 8, 0:T].bitcast(I32), tab_scales[:, 4 * q:4 * q + 4, :].bitcast(I32))
         for q in range(4):
-            queue = nc.scalar if q < 2 else nc.gpsimd
-            queue.dma_start(w8sc[32 * q:32 * q + 8, :].bitcast(I32), w8_scales[:, 4 * q:4 * q + 4, :].bitcast(I32))
-        nc.gpsimd.dma_start(lev[:], level.rearrange("(p t) -> p t", t=PACK))
+            nc.gpsimd.dma_start(w8sc[32 * q:32 * q + 8, :].bitcast(I32), w8_scales[:, 4 * q:4 * q + 4, :].bitcast(I32))
         load_tab(0)
         load_wscales(nc.sync, w4_scales, 0)
         load_tab(1)
+        nc.sync.dma_start(lev[:], level.rearrange("(p t) -> p t", t=PACK))
 
         w4p = keep.tile([P, PASSES * 2 * H], U8, name="w4p", align_bytes=64)
         nc.vector.tensor_copy(
@@ -97,7 +97,7 @@ def tile_list_spectrum_probe_contrast_kernel(
             w4raw[:].bitcast(U16).rearrange("p (a m t) -> p a t m", a=PASSES, t=PACK),
         )
         def gather_scales(c):
-            nc.vector.tensor_copy(vs[c][:], tsc[:].indirect(offsets[:, c * (CH // 16):(c + 1) * (CH // 16)]))
+            nc.vector.tensor_copy(vs[c][:], tsc.indirect(offsets[:, c * (CH // 16):(c + 1) * (CH // 16)]))
             nc.scalar.dma_start(vs1[0:112, c * CH:(c + 1) * CH].bitcast(I32), vs[c][4:116, :].bitcast(I32))
 
         gather_scales(0)
@@ -112,35 +112,37 @@ def tile_list_spectrum_probe_contrast_kernel(
         load_rows(wrraw[1], wr, 1)
         load_rows(wgraw, wg, 0)
         wscp = keep.tile([P, PASSES * H], U8, name="wscp", align_bytes=64)
-        w8scp = turns.tile([P, H], U8, name="w8scp", align_bytes=64, offset=2048)
+        w8scp = keep.tile([P, H], U8, name="w8scp", tag="wsc", align_bytes=64)
 
         def deal_w4_scales():
-            nc.vector.tensor_copy(
-                wscp[:].rearrange("p (a t m) -> p a t m", a=PASSES, t=PACK),
-                wsc[:].rearrange("p (a m t) -> p a t m", a=PASSES, t=PACK),
-            )
+            for a in range(PASSES):
+                nc.gpsimd.tensor_copy(
+                    wscp[:, a * H:(a + 1) * H].rearrange("p (t m) -> p t m", t=PACK),
+                    wsc[:, a * H:(a + 1) * H].rearrange("p (m t) -> p t m", t=PACK),
+                )
 
         def deal_w8():
             nc.vector.tensor_copy(
                 w8p[:].rearrange("p (a t m) -> p a m t", a=PASSES, t=PACK),
                 w8raw[:].rearrange("p (a m t) -> p a m t", a=PASSES, t=PACK),
             )
-            nc.vector.tensor_copy(
+            nc.gpsimd.tensor_copy(
                 w8scp[:].rearrange("p (t m) -> p t m", t=PACK),
                 w8sc[:].rearrange("p (m t) -> p t m", t=PACK),
             )
 
         vw = [
-            [keep.tile([P, CH], U32, name=f"vw{a}_0", align_bytes=64),
-             turns.tile([P, CH], U32, name=f"vw{a}_1", align_bytes=64, offset=(0, 4032)[a])]
-            for a in range(PASSES)
+            [keep.tile([P, CH], U32, name="vw0_0", align_bytes=64),
+             keep.tile([P, CH], U32, name="vw0_1", align_bytes=64)],
+            [keep.tile([P, CH], U32, name="vw1_0", align_bytes=64),
+             turns.tile([P, CH], U32, name="vw1_1", align_bytes=64, offset=61440)],
         ]
 
         def gather(a, c):
             cols = slice(c * (CH // 16), (c + 1) * (CH // 16))
             nc.vector.tensor_copy(vw[a][c][:], tabw[a][:].bitcast(U32).indirect(offsets[:, cols]))
 
-        w1bf = [turns.tile([P, PACK * H], BF16, name=f"w1bf{a}", align_bytes=64, offset=(14336, 24576)[a]) for a in range(PASSES)]
+        w1bf = [turns.tile([P, PACK * H], BF16, name=f"w1bf{a}", align_bytes=64, offset=(8192, 24576)[a]) for a in range(PASSES)]
         w1q = [keep.tile([P, H], U32, name=f"w1q{a}", align_bytes=64) for a in range(PASSES)]
         w1s = [keep.tile([P, H], U8, name=f"w1s{a}", align_bytes=64) for a in range(PASSES)]
 
@@ -238,6 +240,13 @@ def tile_list_spectrum_probe_contrast_kernel(
                 src[:].rearrange("p (j c i) -> p c j i", i=4, j=PACK),
             )
 
+        def cast_rows_gpsimd(dst, src):
+            nc.gpsimd.tensor_scalar(
+                dst.rearrange("p (c j) -> p c j", j=PACK),
+                src[:].rearrange("p (j c) -> p c j", j=PACK),
+                1.0, 0.0, ALU.mult, ALU.add,
+            )
+
         def quant_o(src, col0, lo, hi):
             cols = slice(col0 + lo, col0 + hi)
             nc.vector.quantize_mx(out=oq[:, cols].bitcast(FP8X4), scales=osc[:, cols], in_=src[:, PACK * lo:PACK * hi])
@@ -246,7 +255,7 @@ def tile_list_spectrum_probe_contrast_kernel(
         hsc = keep.tile([P, S], U8, name="hsc", align_bytes=64)
         out2v = out_2[0].rearrange("p s i -> p (s i)").bitcast(I32)
 
-        hbf = [keep.tile([P, CH * PACK], BF16, name=f"hbf{c}", align_bytes=64) for c in range(CHUNKS)]
+        hbf = [keep.tile([P, CH * PACK], BF16, name=f"hbf{c}", tag=f"hbf{c}", align_bytes=64) for c in range(CHUNKS)]
 
         def cast_h(c, lo=0, hi=CH):
             nc.vector.tensor_copy(
@@ -296,24 +305,21 @@ def tile_list_spectrum_probe_contrast_kernel(
 
         gather(0, 0)
         deal_w4_scales()
+        gather(0, 1)
         gather(1, 0)
         for a in range(PASSES):
-            for t in range(2):
+            for t in range(PACK):
                 both_pass(0, t, a)
-        for t in range(2, PACK):
-            both_pass(0, t, 1, 1)
-            both_pass(0, t, 0, 1)
         for t in range(PACK):
             magnitude(0, t)
         deal_w8()
-        gather(0, 1)
         gather(1, 1)
         for t in range(PACK):
             diff[0, t] = psum.tile([P, CH], F32, name=f"bank{4 + t}")
             w8_passes(0, t, True)
         for t in range(PACK):
-            for a in range(PASSES):
-                both_pass(1, t, a)
+            both_pass(1, t, 1, 1)
+            both_pass(1, t, 0, 1)
         invert_all(0)
         for t in range(PACK):
             magnitude(1, t)
@@ -325,7 +331,10 @@ def tile_list_spectrum_probe_contrast_kernel(
         wrbf = turns.tile([P, PASSES * N * PACK], BF16, name="wrbf", align_bytes=64, offset=24576)
         wgbf = keep.tile([P, N * PACK], BF16, name="wgbf", tag="mag1_3", align_bytes=64)
         for a in range(PASSES):
-            cast_rows(wrbf[:, a * N * PACK:(a + 1) * N * PACK], wrraw[a])
+            if a == 0:
+                cast_rows(wrbf[:, 0:N * PACK], wrraw[0])
+            else:
+                cast_rows(wrbf[:, N * PACK:], wrraw[1])
             contrast(0, 2 * a)
             contrast(0, 2 * a + 1)
         quant_o(wrbf, 0, 0, 512)
@@ -335,25 +344,25 @@ def tile_list_spectrum_probe_contrast_kernel(
         invert_all(1)
         cast_rows(wgbf[:], wgraw, nc.scalar.copy)
         for t in range(PACK):
-            open_diff(1, t, t, 1)
+            open_diff(1, t, (0, 4, 5, 6)[t], 1)
             w8_passes(1, t)
             w1_pass(1, t, 0, False, True)
             contrast(1, t)
         for j in range(NT):
-            raw_product(0, j, 4 + j)
+            raw_product(0, j, 1 + j)
         quant_o(wgbf, 768, 0, 256)
         quant_o(wgbf, 768, 256, 384)
         cast_h(1)
         for j in range(NT):
-            readout(0, j, (7, 0, 1)[j])
+            readout(0, j, (7, 0, 4)[j])
         quant_h(1)
         for q in range(4):
             nc.sync.dma_start(out_3[0, 4 * q:4 * q + 4, :].bitcast(I32), hsc[32 * q:32 * q + 4, :].bitcast(I32))
         for j in range(NT):
             finish(0, j)
         for j in range(NT):
-            raw_product(1, j, (2, 3, 7)[j])
+            raw_product(1, j, (5, 6, 7)[j])
         for j in range(NT):
-            readout(1, j, (0, 1, 4)[j])
+            readout(1, j, (0, 4, 1)[j])
         for j in range(NT):
             finish(1, j)

@@ -133,7 +133,7 @@ def tile_list_spectrum_probe_contrast_kernel(
 
         vw = [
             [keep.tile([P, CH], U32, name="vw0_0", align_bytes=64),
-             keep.tile([P, CH], U32, name="vw0_1", align_bytes=64)],
+             turns.tile([P, CH], U32, name="vw0_1", align_bytes=64, offset=59392)],
             [keep.tile([P, CH], U32, name="vw1_0", align_bytes=64),
              turns.tile([P, CH], U32, name="vw1_1", align_bytes=64, offset=61440)],
         ]
@@ -199,7 +199,10 @@ def tile_list_spectrum_probe_contrast_kernel(
                     square(c, t - 1)
 
         w8p = keep.tile([P, PASSES * H], I32, name="w8p", align_bytes=64)
-        hs = [keep.tile([P, PACK, CH], F32, name=f"h{c}", align_bytes=64) for c in range(CHUNKS)]
+        hs = [
+            keep.tile([P, PACK, CH], F32, name="h0", align_bytes=64),
+            turns.tile([P, PACK, CH], F32, name="h1", align_bytes=64, offset=23552),
+        ]
         out1v = out_1.rearrange("(p t) s -> p t s", t=PACK)
 
         diff = {}
@@ -255,7 +258,10 @@ def tile_list_spectrum_probe_contrast_kernel(
         hsc = keep.tile([P, S], U8, name="hsc", align_bytes=64)
         out2v = out_2[0].rearrange("p s i -> p (s i)").bitcast(I32)
 
-        hbf = [keep.tile([P, CH * PACK], BF16, name=f"hbf{c}", tag=f"hbf{c}", align_bytes=64) for c in range(CHUNKS)]
+        hbf = [
+            turns.tile([P, CH * PACK], BF16, name="hbf0", align_bytes=64, offset=20480),
+            keep.tile([P, CH * PACK], BF16, name="hbf1", align_bytes=64),
+        ]
 
         def cast_h(c, lo=0, hi=CH):
             nc.vector.tensor_copy(
@@ -305,7 +311,6 @@ def tile_list_spectrum_probe_contrast_kernel(
 
         gather(0, 0)
         deal_w4_scales()
-        gather(0, 1)
         gather(1, 0)
         for a in range(PASSES):
             for t in range(PACK):
@@ -313,13 +318,14 @@ def tile_list_spectrum_probe_contrast_kernel(
         for t in range(PACK):
             magnitude(0, t)
         deal_w8()
+        gather(0, 1)
         gather(1, 1)
         for t in range(PACK):
             diff[0, t] = psum.tile([P, CH], F32, name=f"bank{4 + t}")
             w8_passes(0, t, True)
-        for t in range(PACK):
-            both_pass(1, t, 1, 1)
-            both_pass(1, t, 0, 1)
+        for a in range(PASSES):
+            for t in range(PACK):
+                both_pass(1, t, a)
         invert_all(0)
         for t in range(PACK):
             magnitude(1, t)
@@ -329,20 +335,17 @@ def tile_list_spectrum_probe_contrast_kernel(
             for t in range(PACK):
                 w1_pass(0, t, a, False, a == PASSES - 1)
         wrbf = turns.tile([P, PASSES * N * PACK], BF16, name="wrbf", align_bytes=64, offset=24576)
-        wgbf = keep.tile([P, N * PACK], BF16, name="wgbf", tag="mag1_3", align_bytes=64)
-        for a in range(PASSES):
-            if a == 0:
-                cast_rows(wrbf[:, 0:N * PACK], wrraw[0])
-            else:
-                cast_rows(wrbf[:, N * PACK:], wrraw[1])
-            contrast(0, 2 * a)
-            contrast(0, 2 * a + 1)
-        quant_o(wrbf, 0, 0, 512)
+        wgbf = turns.tile([P, N * PACK], BF16, name="wgbf", align_bytes=64, offset=20480)
+        cast_rows(wrbf[:, 0:N * PACK], wrraw[0])
+        cast_rows_gpsimd(wrbf[:, N * PACK:], wrraw[1])
+        for t in range(PACK):
+            contrast(0, t)
         cast_h(0)
+        quant_o(wrbf, 0, 0, 512)
         quant_o(wrbf, 0, 512, 768)
         quant_h(0)
         invert_all(1)
-        cast_rows(wgbf[:], wgraw, nc.scalar.copy)
+        cast_rows_gpsimd(wgbf[:], wgraw)
         for t in range(PACK):
             open_diff(1, t, (0, 4, 5, 6)[t], 1)
             w8_passes(1, t)

@@ -38,8 +38,8 @@ def tile_list_spectrum_probe_contrast_kernel(
         psum = ctx.enter_context(tc.psum_pool(name="psum", bufs=1))
 
         offsets = keep.tile([P, S // 16], U16, name="offsets")
-        early = turns.tile([P, 38912], U8, name="early", align_bytes=64, offset=22528)
-        tsc = early[:, 0:T]
+        tsc_tile = keep.tile([P, T], U8, name="tsc", align_bytes=64)
+        tsc = tsc_tile[:]
         wsc = keep.tile([P, PASSES * H], U8, name="wsc", tag="wsc", align_bytes=64)
         vs1 = keep.tile([P, S], U8, name="vs1", align_bytes=64)
         warm = keep.tile([P, 1], F32, name="warm")
@@ -83,7 +83,7 @@ def tile_list_spectrum_probe_contrast_kernel(
             w4_words.bitcast(I32).rearrange("a p c -> p a c"),
         )
         for q in range(4):
-            nc.sync.dma_start(early[32 * q:32 * q + 8, 0:T].bitcast(I32), tab_scales[:, 4 * q:4 * q + 4, :].bitcast(I32))
+            nc.sync.dma_start(tsc_tile[32 * q:32 * q + 8, :].bitcast(I32), tab_scales[:, 4 * q:4 * q + 4, :].bitcast(I32))
         for q in range(4):
             nc.gpsimd.dma_start(w8sc[32 * q:32 * q + 8, :].bitcast(I32), w8_scales[:, 4 * q:4 * q + 4, :].bitcast(I32))
         load_tab(0)
@@ -102,12 +102,12 @@ def tile_list_spectrum_probe_contrast_kernel(
 
         gather_scales(0)
         gather_scales(1)
+        load_rows(w1raw[0], w1, 0)
+        load_rows(w1raw[1], w1, 1)
         nc.sync.dma_start(
             w8raw[:].rearrange("p (a c) -> p a c", a=PASSES),
             w8_words.rearrange("a p c i -> p a (c i)").bitcast(I32),
         )
-        load_rows(w1raw[0], w1, 0)
-        load_rows(w1raw[1], w1, 1)
         load_rows(wrraw[0], wr, 0)
         load_rows(wrraw[1], wr, 1)
         load_rows(wgraw, wg, 0)
@@ -133,9 +133,9 @@ def tile_list_spectrum_probe_contrast_kernel(
 
         vw = [
             [keep.tile([P, CH], U32, name="vw0_0", align_bytes=64),
-             turns.tile([P, CH], U32, name="vw0_1", align_bytes=64, offset=59392)],
+             keep.tile([P, CH], U32, name="vw0_1", align_bytes=64)],
             [keep.tile([P, CH], U32, name="vw1_0", align_bytes=64),
-             turns.tile([P, CH], U32, name="vw1_1", align_bytes=64, offset=61440)],
+             keep.tile([P, CH], U32, name="vw1_1", align_bytes=64)],
         ]
 
         def gather(a, c):
@@ -188,7 +188,7 @@ def tile_list_spectrum_probe_contrast_kernel(
             nc.scalar.activation(out=roots[c, t][:], in_=mags[c, t][:], func=ACT.Abs_reciprocal_sqrt, bias=lev[:, t:t + 1])
 
         def square(c, t):
-            recip[c, t, 0] = keep.tile([P, CH], F32, name=f"recip{c}_{t}", align_bytes=64)
+            recip[c, t, 0] = keep.tile([P, CH], F32, name=f"recip{c}_{t}", tag=f"recip{c}_{t}", align_bytes=64)
             nc.scalar.activation(out=recip[c, t, 0][:], in_=roots[c, t][:], func=ACT.Square)
 
         def invert_all(c):
@@ -243,13 +243,6 @@ def tile_list_spectrum_probe_contrast_kernel(
                 src[:].rearrange("p (j c i) -> p c j i", i=4, j=PACK),
             )
 
-        def cast_rows_gpsimd(dst, src):
-            nc.gpsimd.tensor_scalar(
-                dst.rearrange("p (c j) -> p c j", j=PACK),
-                src[:].rearrange("p (j c) -> p c j", j=PACK),
-                1.0, 0.0, ALU.mult, ALU.add,
-            )
-
         def quant_o(src, col0, lo, hi):
             cols = slice(col0 + lo, col0 + hi)
             nc.vector.quantize_mx(out=oq[:, cols].bitcast(FP8X4), scales=osc[:, cols], in_=src[:, PACK * lo:PACK * hi])
@@ -276,6 +269,11 @@ def tile_list_spectrum_probe_contrast_kernel(
                 whole = slice(c * CH, (c + 1) * CH)
                 nc.sync.dma_start(out2v[:, whole], hq[:, whole].bitcast(I32))
 
+        def pieces(c, j):
+            if (c, j) == (CHUNKS - 1, NT - 1):
+                return ((0, HALF), (HALF, CH))
+            return ((0, CH),)
+
         raws = {}
         sigs = {}
 
@@ -301,51 +299,56 @@ def tile_list_spectrum_probe_contrast_kernel(
                 start=True, stop=True,
             )
             sigs[c, j] = keep.tile([P, CH], F32, name=f"sig{c}_{j}")
-            nc.scalar.activation(out=sigs[c, j][:], in_=gate[:], func=ACT.Sigmoid)
+            for lo, hi in pieces(c, j):
+                nc.scalar.activation(out=sigs[c, j][:, lo:hi], in_=gate[:, lo:hi], func=ACT.Sigmoid)
 
         def finish(c, j):
-            cols = slice(c * CH, (c + 1) * CH)
             y = keep.tile([P, CH], F32, name=f"y{c}_{j}")
-            nc.vector.tensor_tensor(y[:], raws[c, j][:], sigs[c, j][:], ALU.mult)
-            nc.sync.dma_start(out_0[j * P:(j + 1) * P, cols], y[:])
+            for lo, hi in pieces(c, j):
+                nc.vector.tensor_tensor(y[:, lo:hi], raws[c, j][:, lo:hi], sigs[c, j][:, lo:hi], ALU.mult)
+                nc.sync.dma_start(out_0[j * P:(j + 1) * P, c * CH + lo:c * CH + hi], y[:, lo:hi])
 
         gather(0, 0)
         deal_w4_scales()
+        gather(0, 1)
         gather(1, 0)
         for a in range(PASSES):
             for t in range(PACK):
                 both_pass(0, t, a)
         for t in range(PACK):
             magnitude(0, t)
-        deal_w8()
-        gather(0, 1)
         gather(1, 1)
         for t in range(PACK):
-            diff[0, t] = psum.tile([P, CH], F32, name=f"bank{4 + t}")
-            w8_passes(0, t, True)
-        for a in range(PASSES):
-            for t in range(PACK):
-                both_pass(1, t, a)
+            both_pass(1, t, 1, 1)
+            both_pass(1, t, 0, 1)
         invert_all(0)
         for t in range(PACK):
             magnitude(1, t)
-        for a in range(PASSES):
-            cast_w1(a, False)
-            quant_w1(a)
-            for t in range(PACK):
-                w1_pass(0, t, a, False, a == PASSES - 1)
-        wrbf = turns.tile([P, PASSES * N * PACK], BF16, name="wrbf", align_bytes=64, offset=24576)
-        wgbf = turns.tile([P, N * PACK], BF16, name="wgbf", align_bytes=64, offset=20480)
-        cast_rows(wrbf[:, 0:N * PACK], wrraw[0])
-        cast_rows_gpsimd(wrbf[:, N * PACK:], wrraw[1])
+        cast_w1(0, False)
+        quant_w1(0)
+        for t in range(PACK):
+            open_diff(0, t, 4 + t, 0)
+        cast_w1(1, False)
+        deal_w8()
+        quant_w1(1)
+        for t in range(PACK):
+            w8_passes(0, t)
+            w1_pass(0, t, 1, False, True)
+        wrbf = turns.tile([P, N * PACK], BF16, name="wrbf", align_bytes=64, offset=24576)
+        cast_rows(wrbf[:], wrraw[0])
         for t in range(PACK):
             contrast(0, t)
+        wrbf1 = keep.tile([P, N * PACK], BF16, name="wrbf1", tag="recip0_0", align_bytes=64)
+        cast_rows(wrbf1[:], wrraw[1])
         cast_h(0)
-        quant_o(wrbf, 0, 0, 512)
-        quant_o(wrbf, 0, 512, 768)
+        quant_o(wrbf, 0, 0, 256)
+        quant_o(wrbf, 0, 256, 384)
         quant_h(0)
+        quant_o(wrbf1, N, 0, 256)
+        quant_o(wrbf1, N, 256, 384)
         invert_all(1)
-        cast_rows_gpsimd(wgbf[:], wgraw)
+        wgbf = keep.tile([P, N * PACK], BF16, name="wgbf", tag="mag1_3", align_bytes=64)
+        cast_rows(wgbf[:], wgraw, nc.scalar.copy)
         for t in range(PACK):
             open_diff(1, t, (0, 4, 5, 6)[t], 1)
             w8_passes(1, t)

@@ -82,8 +82,11 @@ def tile_list_spectrum_probe_contrast_kernel(
             w4raw[:].bitcast(I32).rearrange("p (a c) -> p a c", a=PASSES),
             w4_words.bitcast(I32).rearrange("a p c -> p a c"),
         )
-        for q in range(4):
-            nc.sync.dma_start(tsc_tile[32 * q:32 * q + 8, :].bitcast(I32), tab_scales[:, 4 * q:4 * q + 4, :].bitcast(I32))
+        for r in range(4):
+            nc.sync.dma_start(
+                tsc_tile[r:P:16, :].bitcast(I32),
+                tab_scales.bitcast(I32).rearrange("a (q r) c -> r q a c", r=4)[r],
+            )
         for q in range(4):
             nc.gpsimd.dma_start(w8sc[32 * q:32 * q + 8, :].bitcast(I32), w8_scales[:, 4 * q:4 * q + 4, :].bitcast(I32))
         load_tab(0)
@@ -98,7 +101,7 @@ def tile_list_spectrum_probe_contrast_kernel(
         )
         def gather_scales(c):
             nc.vector.tensor_copy(vs[c][:], tsc.indirect(offsets[:, c * (CH // 16):(c + 1) * (CH // 16)]))
-            nc.scalar.dma_start(vs1[0:112, c * CH:(c + 1) * CH].bitcast(I32), vs[c][4:116, :].bitcast(I32))
+            nc.scalar.dma_start(vs1[0:112, c * CH:(c + 1) * CH].bitcast(I32), vs[c][16:128, :].bitcast(I32))
 
         gather_scales(0)
         gather_scales(1)
@@ -158,7 +161,7 @@ def tile_list_spectrum_probe_contrast_kernel(
             nc.vector.quantize_mx(out=w1q[a][:].bitcast(FP8X4), scales=w1s[a][:], in_=w1bf[a][:])
 
         def vscale(a, c):
-            return vs[c][4 * a:, :]
+            return vs[c][:] if a == 0 else vs1[:, c * CH:(c + 1) * CH]
 
         recip = {}
         mags = {}

@@ -240,15 +240,23 @@ def tile_list_spectrum_probe_contrast_kernel(
         oq = keep.tile([P, (PASSES + 1) * N], U32, name="oq", align_bytes=64)
         osc = keep.tile([P, (PASSES + 1) * N], U8, name="osc", align_bytes=64)
 
-        def cast_rows(dst, src, copy=nc.vector.tensor_copy):
+        def cast_rows(dst, src, copy=nc.vector.tensor_copy, lo=0, hi=N):
             copy(
                 dst.rearrange("p (c i j) -> p c j i", i=4, j=PACK),
-                src[:].rearrange("p (j c i) -> p c j i", i=4, j=PACK),
+                src[:].rearrange("p (j c) -> p j c", j=PACK)[:, :, lo:hi].rearrange("p j (c i) -> p c j i", i=4),
             )
 
-        def quant_o(src, col0, lo, hi):
+        def cast_rows_gpsimd(dst, src, lo, hi):
+            nc.gpsimd.tensor_scalar(
+                dst.rearrange("p (c j) -> p c j", j=PACK),
+                src[:].rearrange("p (j c) -> p c j", j=PACK)[:, lo:hi, :],
+                1.0, 0.0, ALU.mult, ALU.add,
+            )
+
+        def quant_o(src, col0, lo, hi, whole=False):
             cols = slice(col0 + lo, col0 + hi)
-            nc.vector.quantize_mx(out=oq[:, cols].bitcast(FP8X4), scales=osc[:, cols], in_=src[:, PACK * lo:PACK * hi])
+            part = src[:] if whole else src[:, PACK * lo:PACK * hi]
+            nc.vector.quantize_mx(out=oq[:, cols].bitcast(FP8X4), scales=osc[:, cols], in_=part)
 
         hq = keep.tile([P, S], U32, name="hq", align_bytes=64)
         hsc = keep.tile([P, S], U8, name="hsc", align_bytes=64)
@@ -259,8 +267,8 @@ def tile_list_spectrum_probe_contrast_kernel(
             keep.tile([P, CH * PACK], BF16, name="hbf1", align_bytes=64),
         ]
 
-        def cast_h(c, lo=0, hi=CH):
-            nc.vector.tensor_copy(
+        def cast_h(c, lo=0, hi=CH, copy=nc.vector.tensor_copy):
+            copy(
                 hbf[c][:, PACK * lo:PACK * hi].rearrange("p (c i t) -> p c t i", i=4, t=PACK),
                 hs[c][:, :, lo:hi].rearrange("p t (c i) -> p c t i", i=4),
             )
@@ -341,7 +349,7 @@ def tile_list_spectrum_probe_contrast_kernel(
         cast_rows(wrbf[:], wrraw[0])
         for t in range(PACK):
             contrast(0, t)
-        wrbf1 = keep.tile([P, N * PACK], BF16, name="wrbf1", tag="recip0_0", align_bytes=64)
+        wrbf1 = turns.tile([P, N * PACK], BF16, name="wrbf1", align_bytes=64, offset=12288)
         cast_rows(wrbf1[:], wrraw[1])
         cast_h(0)
         quant_o(wrbf, 0, 0, 256)
@@ -350,8 +358,12 @@ def tile_list_spectrum_probe_contrast_kernel(
         quant_o(wrbf1, N, 0, 256)
         quant_o(wrbf1, N, 256, 384)
         invert_all(1)
-        wgbf = keep.tile([P, N * PACK], BF16, name="wgbf", tag="mag1_3", align_bytes=64)
-        cast_rows(wgbf[:], wgraw, nc.scalar.copy)
+        warm3 = keep.tile([P, 1], F32, name="warm3")
+        nc.scalar.activation(out=warm3[:], in_=recip[1, PACK - 1, 0][:, 0:1], func=ACT.Sigmoid)
+        wgbfa = turns.tile([P, 256 * PACK], BF16, name="wgbfa", align_bytes=64, offset=12288)
+        wgbfb = turns.tile([P, 128 * PACK], BF16, name="wgbfb", align_bytes=64, offset=13312 + 1024)
+        cast_rows_gpsimd(wgbfa[:], wgraw, 0, 256)
+        cast_rows_gpsimd(wgbfb[:], wgraw, 256, 384)
         for t in range(PACK):
             open_diff(1, t, (0, 4, 5, 6)[t], 1)
             w8_passes(1, t)
@@ -359,9 +371,10 @@ def tile_list_spectrum_probe_contrast_kernel(
             contrast(1, t)
         for j in range(NT):
             raw_product(0, j, 1 + j)
-        quant_o(wgbf, 768, 0, 256)
-        quant_o(wgbf, 768, 256, 384)
-        cast_h(1)
+        cast_h(1, 0, HALF)
+        cast_h(1, HALF, CH, nc.scalar.copy)
+        quant_o(wgbfa, 768, 0, 256, True)
+        quant_o(wgbfb, 768, 256, 384, True)
         for j in range(NT):
             readout(0, j, (7, 0, 4)[j])
         quant_h(1)

@@ -24,6 +24,8 @@ CH = 512
 CHUNKS = S // CH
 NT = N // P
 HALF = CH // 2
+SPLIT = 288
+WG_SPLIT = 320
 
 
 def tile_list_spectrum_probe_contrast_kernel(
@@ -58,7 +60,7 @@ def tile_list_spectrum_probe_contrast_kernel(
 
         nc.sync.dma_start(offsets[:], offs)
         tabw = [turns.tile([P, T], I32, name=f"tabw{a}", align_bytes=64, offset=(0, 8192)[a]) for a in range(PASSES)]
-        w1raw = [turns.tile([P, PACK * H], F32, name=f"w1raw{a}", align_bytes=64, offset=(24576, 32768)[a]) for a in range(PASSES)]
+        w1raw = [turns.tile([P, PACK * H], F32, name=f"w1raw{a}", align_bytes=64, offset=24576) for a in range(1)]
         wrraw = [turns.tile([P, PACK * N], F32, name=f"wrraw{a}", align_bytes=64, offset=(40960, 47104)[a]) for a in range(PASSES)]
         wgraw = turns.tile([P, PACK * N], F32, name="wgraw", align_bytes=64, offset=53248)
         w4raw = keep.tile([P, PASSES * 2 * H], U8, name="w4raw", align_bytes=64)
@@ -106,11 +108,16 @@ def tile_list_spectrum_probe_contrast_kernel(
         gather_scales(0)
         gather_scales(1)
         load_rows(w1raw[0], w1, 0)
-        load_rows(w1raw[1], w1, 1)
         nc.sync.dma_start(
             w8raw[:].rearrange("p (a c) -> p a c", a=PASSES),
             w8_words.rearrange("a p c i -> p a (c i)").bitcast(I32),
         )
+        w1half = [turns.tile([P, PACK, H // 2], F32, name=f"w1half{u}", align_bytes=64, offset=32768 + 4096 * u) for u in range(2)]
+        for u in range(2):
+            nc.sync.dma_start(
+                w1half[u][:],
+                w1[KP:2 * KP, u * (H // 2):(u + 1) * (H // 2)].rearrange("(p j) c -> p j c", j=PACK),
+            )
         load_rows(wrraw[0], wr, 0)
         load_rows(wrraw[1], wr, 1)
         load_rows(wgraw, wg, 0)
@@ -141,9 +148,9 @@ def tile_list_spectrum_probe_contrast_kernel(
              keep.tile([P, CH], U32, name="vw1_1", align_bytes=64)],
         ]
 
-        def gather(a, c):
-            cols = slice(c * (CH // 16), (c + 1) * (CH // 16))
-            nc.vector.tensor_copy(vw[a][c][:], tabw[a][:].bitcast(U32).indirect(offsets[:, cols]))
+        def gather(a, c, lo=0, hi=CH):
+            cols = slice((c * CH + lo) // 16, (c * CH + hi) // 16)
+            nc.vector.tensor_copy(vw[a][c][:, lo:hi], tabw[a][:].bitcast(U32).indirect(offsets[:, cols]))
 
         w1bf = [turns.tile([P, PACK * H], BF16, name=f"w1bf{a}", align_bytes=64, offset=(8192, 24576)[a]) for a in range(PASSES)]
         w1q = [keep.tile([P, H], U32, name=f"w1q{a}", align_bytes=64) for a in range(PASSES)]
@@ -156,6 +163,11 @@ def tile_list_spectrum_probe_contrast_kernel(
                 nc.scalar.activation(out=dst, in_=src, func=ACT.Copy, scale=-1.0)
             else:
                 nc.vector.tensor_scalar(dst, src, -1.0, None, ALU.mult)
+
+        def cast_w1_half(u):
+            dst = w1bf[1][:].rearrange("p (t m j) -> p m j t", t=PACK, j=PACK)[:, u * 64:(u + 1) * 64, :, :]
+            src = w1half[u][:].rearrange("p j (m t) -> p m j t", t=PACK)
+            nc.vector.tensor_scalar(dst, src, -1.0, None, ALU.mult)
 
         def quant_w1(a):
             nc.vector.quantize_mx(out=w1q[a][:].bitcast(FP8X4), scales=w1s[a][:], in_=w1bf[a][:])
@@ -170,7 +182,7 @@ def tile_list_spectrum_probe_contrast_kernel(
 
         def both_pass(c, t, a, first=0):
             if a == first:
-                sums[c, t] = psum.tile([P, CH], F32, name=f"bank{t}")
+                sums[c, t] = psum.tile([P, CH], F32, name=f"bank{((0, 1, 2, 3), (0, 1, 4, 5))[c][t]}")
             col = a * H + t * P
             plane = vs[c][:] if a == 0 else vs1[:, c * CH:(c + 1) * CH]
             nc.tensor.matmul_mx(
@@ -179,6 +191,26 @@ def tile_list_spectrum_probe_contrast_kernel(
                 rhs=vw[a][c][:].bitcast(FP8X4), rhs_scale=plane,
                 start=(a == first), stop=(a != first),
             )
+
+        halves = {}
+
+        def half_pass(t, u, a):
+            if a == 0:
+                halves[t, u] = psum.tile([P, CH], F32, name=f"bank{t + 4 * (1 - u)}")
+            col = a * H + t * P
+            for i in range(2):
+                cols = slice(u * HALF + i * P, u * HALF + (i + 1) * P)
+                nc.tensor.matmul_mx(
+                    out=halves[t, u][:, i * P:(i + 1) * P],
+                    lhsT=w4p[:, 2 * col:2 * (col + P)].bitcast(FP4X4), lhsT_scale=wscp[:, col:col + P],
+                    rhs=vw[a][0][:, cols].bitcast(FP8X4), rhs_scale=vscale(a, 0)[:, cols],
+                    start=(a == 0 and i == 0), stop=(a == 1 and i == 1),
+                )
+
+        def half_magnitude(t, u):
+            if u == 0:
+                mags[0, t] = keep.tile([P, CH], F32, name=f"mag0_{t}", tag=f"mag0_{t}", align_bytes=64)
+            nc.scalar.activation(out=mags[0, t][:, u * HALF:(u + 1) * HALF], in_=halves[t, u][:, 0:HALF], func=ACT.Abs)
 
         def magnitude(c, t):
             mags[c, t] = keep.tile([P, CH], F32, name=f"mag{c}_{t}", tag=f"mag{c}_{t}", align_bytes=64)
@@ -191,7 +223,10 @@ def tile_list_spectrum_probe_contrast_kernel(
             nc.scalar.activation(out=roots[c, t][:], in_=mags[c, t][:], func=ACT.Abs_reciprocal_sqrt, bias=lev[:, t:t + 1])
 
         def square(c, t):
-            recip[c, t, 0] = keep.tile([P, CH], F32, name=f"recip{c}_{t}", tag=f"recip{c}_{t}", align_bytes=64)
+            if (c, t) == (0, PACK - 1):
+                recip[c, t, 0] = turns.tile([P, CH], F32, name="recip0_3", align_bytes=64, offset=13312)
+            else:
+                recip[c, t, 0] = keep.tile([P, CH], F32, name=f"recip{c}_{t}", tag=f"recip{c}_{t}", align_bytes=64)
             nc.scalar.activation(out=recip[c, t, 0][:], in_=roots[c, t][:], func=ACT.Square)
 
         def invert_all(c):
@@ -319,72 +354,107 @@ def tile_list_spectrum_probe_contrast_kernel(
                 nc.vector.tensor_tensor(y[:, lo:hi], raws[c, j][:, lo:hi], sigs[c, j][:, lo:hi], ALU.mult)
                 nc.sync.dma_start(out_0[j * P:(j + 1) * P, c * CH + lo:c * CH + hi], y[:, lo:hi])
 
-        gather(0, 0)
+        gather(0, 0, 0, HALF)
+        gather(0, 0, HALF, CH)
         deal_w4_scales()
         gather(0, 1)
-        gather(1, 0)
+        gather(1, 0, 0, HALF)
+        gather(1, 0, HALF, CH)
         for a in range(PASSES):
-            for t in range(PACK):
+            for u in range(2):
+                for t in range(2):
+                    half_pass(t, u, a)
+            for t in range(2, PACK):
                 both_pass(0, t, a)
-        for t in range(PACK):
-            magnitude(0, t)
+        for u in range(2):
+            for t in range(2):
+                half_magnitude(t, u)
+        inverse_root(0, 0)
+        magnitude(0, 2)
+        inverse_root(0, 1)
+        magnitude(0, 3)
         gather(1, 1)
-        for t in range(PACK):
+        for t in range(2):
             both_pass(1, t, 1, 1)
             both_pass(1, t, 0, 1)
-        invert_all(0)
-        for t in range(PACK):
-            magnitude(1, t)
+        square(0, 0)
+        inverse_root(0, 2)
+        square(0, 1)
+        inverse_root(0, 3)
+        square(0, 2)
+        square(0, 3)
+        magnitude(1, 0)
+        magnitude(1, 1)
+        inverse_root(1, 0)
         cast_w1(0, False)
-        quant_w1(0)
-        for t in range(PACK):
-            open_diff(0, t, 4 + t, 0)
-        cast_w1(1, False)
         deal_w8()
+        quant_w1(0)
+        for t in range(PACK - 1):
+            diff[0, t] = psum.tile([P, CH], F32, name=f"bank{4 + t}")
+            w8_passes(0, t, True)
+            w1_pass(0, t, 0, False, False)
+        cast_w1_half(0)
+        cast_w1_half(1)
         quant_w1(1)
-        for t in range(PACK):
-            w8_passes(0, t)
+        for t in range(PACK - 1):
             w1_pass(0, t, 1, False, True)
-        wrbf = turns.tile([P, N * PACK], BF16, name="wrbf", align_bytes=64, offset=24576)
-        cast_rows(wrbf[:], wrraw[0])
+        open_diff(0, PACK - 1, 7, 1)
+        w8_passes(0, PACK - 1)
+        w1_pass(0, PACK - 1, 0, False, True)
+        wrbfa = turns.tile([P, 256 * PACK], BF16, name="wrbfa", align_bytes=64, offset=24576)
+        cast_rows_gpsimd(wrbfa[:], wrraw[0], 0, 256)
         for t in range(PACK):
             contrast(0, t)
-        wrbf1 = turns.tile([P, N * PACK], BF16, name="wrbf1", align_bytes=64, offset=12288)
+        for t in range(2, PACK):
+            both_pass(1, t, 1, 1)
+            both_pass(1, t, 0, 1)
+        magnitude(1, 2)
+        inverse_root(1, 1)
+        magnitude(1, 3)
+        square(1, 0)
+        inverse_root(1, 2)
+        square(1, 1)
+        inverse_root(1, 3)
+        square(1, 2)
+        square(1, 3)
+        wrbfb = turns.tile([P, 128 * PACK], BF16, name="wrbfb", align_bytes=64, offset=14336)
+        cast_rows(wrbfb[:], wrraw[0], nc.vector.tensor_copy, 256, 384)
+        wrbf1 = turns.tile([P, N * PACK], BF16, name="wrbf1", align_bytes=64, offset=11264)
         cast_rows(wrbf1[:], wrraw[1])
         cast_h(0)
-        quant_o(wrbf, 0, 0, 256)
-        quant_o(wrbf, 0, 256, 384)
+        quant_o(wrbfa, 0, 0, 256, True)
+        quant_o(wrbfb, 0, 256, 384, True)
         quant_h(0)
         quant_o(wrbf1, N, 0, 256)
         quant_o(wrbf1, N, 256, 384)
-        invert_all(1)
+        wgbf = turns.tile([P, N * PACK], BF16, name="wgbf", align_bytes=64, offset=11264)
+        cast_rows_gpsimd(wgbf[:, :WG_SPLIT * PACK], wgraw, 0, WG_SPLIT)
+        cast_rows(wgbf[:, WG_SPLIT * PACK:], wgraw, nc.scalar.copy, WG_SPLIT, N)
         warm3 = keep.tile([P, 1], F32, name="warm3")
         nc.scalar.activation(out=warm3[:], in_=recip[1, PACK - 1, 0][:, 0:1], func=ACT.Sigmoid)
-        wgbfa = turns.tile([P, 256 * PACK], BF16, name="wgbfa", align_bytes=64, offset=12288)
-        wgbfb = turns.tile([P, 128 * PACK], BF16, name="wgbfb", align_bytes=64, offset=13312 + 1024)
-        cast_rows_gpsimd(wgbfa[:], wgraw, 0, 256)
-        cast_rows_gpsimd(wgbfb[:], wgraw, 256, 384)
         for t in range(PACK):
-            open_diff(1, t, (0, 4, 5, 6)[t], 1)
+            open_diff(1, t, (0, 1, 6, 7)[t], 1)
             w8_passes(1, t)
             w1_pass(1, t, 0, False, True)
             contrast(1, t)
         for j in range(NT):
-            raw_product(0, j, 1 + j)
-        cast_h(1, 0, HALF)
-        cast_h(1, HALF, CH, nc.scalar.copy)
-        quant_o(wgbfa, 768, 0, 256, True)
-        quant_o(wgbfb, 768, 256, 384, True)
+            raw_product(0, j, 2 + j)
+        raw_product(1, 0, 5)
+        quant_o(wgbf, 768, 0, 256)
+        quant_o(wgbf, 768, 256, 384)
+        cast_h(1, 0, SPLIT)
+        cast_h(1, SPLIT, CH, nc.scalar.copy)
         for j in range(NT):
-            readout(0, j, (7, 0, 4)[j])
+            readout(0, j, (0, 1, 6)[j])
         quant_h(1)
         for q in range(4):
             nc.sync.dma_start(out_3[0, 4 * q:4 * q + 4, :].bitcast(I32), hsc[32 * q:32 * q + 4, :].bitcast(I32))
         for j in range(NT):
             finish(0, j)
-        for j in range(NT):
-            raw_product(1, j, (5, 6, 7)[j])
-        for j in range(NT):
-            readout(1, j, (0, 4, 1)[j])
+        raw_product(1, 1, 0)
+        readout(1, 0, 7)
+        readout(1, 1, 1)
+        raw_product(1, 2, 6)
+        readout(1, 2, 2)
         for j in range(NT):
             finish(1, j)

@@ -60,11 +60,11 @@ def tile_list_spectrum_probe_contrast_kernel(
 
         nc.sync.dma_start(offsets[:], offs)
         tabw = [turns.tile([P, T], I32, name=f"tabw{a}", align_bytes=64, offset=(0, 8192)[a]) for a in range(PASSES)]
-        w1raw = [turns.tile([P, PACK * H], F32, name=f"w1raw{a}", align_bytes=64, offset=24576) for a in range(1)]
+        w1raw = [turns.tile([P, PACK * H], F32, name=f"w1raw{a}", align_bytes=64, offset=(24576, 32768)[a]) for a in range(PASSES)]
         wrraw = [turns.tile([P, PACK * N], F32, name=f"wrraw{a}", align_bytes=64, offset=(40960, 47104)[a]) for a in range(PASSES)]
         wgraw = turns.tile([P, PACK * N], F32, name="wgraw", align_bytes=64, offset=53248)
         w4raw = keep.tile([P, PASSES * 2 * H], U8, name="w4raw", align_bytes=64)
-        w8raw = turns.tile([P, PASSES * H], I32, name="w8raw", align_bytes=64, offset=59392)
+        w8raw = [keep.tile([P, H], I32, name=f"w8raw{a}", align_bytes=64) for a in range(PASSES)]
         lev = keep.tile([P, PACK], F32, name="lev")
 
         def load_tab(a):
@@ -108,16 +108,9 @@ def tile_list_spectrum_probe_contrast_kernel(
         gather_scales(0)
         gather_scales(1)
         load_rows(w1raw[0], w1, 0)
-        nc.sync.dma_start(
-            w8raw[:].rearrange("p (a c) -> p a c", a=PASSES),
-            w8_words.rearrange("a p c i -> p a (c i)").bitcast(I32),
-        )
-        w1half = [turns.tile([P, PACK, H // 2], F32, name=f"w1half{u}", align_bytes=64, offset=32768 + 4096 * u) for u in range(2)]
-        for u in range(2):
-            nc.sync.dma_start(
-                w1half[u][:],
-                w1[KP:2 * KP, u * (H // 2):(u + 1) * (H // 2)].rearrange("(p j) c -> p j c", j=PACK),
-            )
+        nc.sync.dma_start(w8raw[0][:], w8_words[0].rearrange("p c i -> p (c i)").bitcast(I32))
+        load_rows(w1raw[1], w1, 1)
+        nc.sync.dma_start(w8raw[1][:], w8_words[1].rearrange("p c i -> p (c i)").bitcast(I32))
         load_rows(wrraw[0], wr, 0)
         load_rows(wrraw[1], wr, 1)
         load_rows(wgraw, wg, 0)
@@ -131,11 +124,13 @@ def tile_list_spectrum_probe_contrast_kernel(
                     wsc[:, a * H:(a + 1) * H].rearrange("p (m t) -> p t m", t=PACK),
                 )
 
-        def deal_w8():
+        def deal_w8(a):
             nc.vector.tensor_copy(
-                w8p[:].rearrange("p (a t m) -> p a m t", a=PASSES, t=PACK),
-                w8raw[:].rearrange("p (a m t) -> p a m t", a=PASSES, t=PACK),
+                w8p[a][:].rearrange("p (t m) -> p m t", t=PACK),
+                w8raw[a][:].rearrange("p (m t) -> p m t", t=PACK),
             )
+
+        def deal_w8_scales():
             nc.gpsimd.tensor_copy(
                 w8scp[:].rearrange("p (t m) -> p t m", t=PACK),
                 w8sc[:].rearrange("p (m t) -> p t m", t=PACK),
@@ -164,11 +159,6 @@ def tile_list_spectrum_probe_contrast_kernel(
             else:
                 nc.vector.tensor_scalar(dst, src, -1.0, None, ALU.mult)
 
-        def cast_w1_half(u):
-            dst = w1bf[1][:].rearrange("p (t m j) -> p m j t", t=PACK, j=PACK)[:, u * 64:(u + 1) * 64, :, :]
-            src = w1half[u][:].rearrange("p j (m t) -> p m j t", t=PACK)
-            nc.vector.tensor_scalar(dst, src, -1.0, None, ALU.mult)
-
         def quant_w1(a):
             nc.vector.quantize_mx(out=w1q[a][:].bitcast(FP8X4), scales=w1s[a][:], in_=w1bf[a][:])
 
@@ -182,7 +172,7 @@ def tile_list_spectrum_probe_contrast_kernel(
 
         def both_pass(c, t, a, first=0):
             if a == first:
-                sums[c, t] = psum.tile([P, CH], F32, name=f"bank{((0, 1, 2, 3), (0, 1, 4, 5))[c][t]}")
+                sums[c, t] = psum.tile([P, CH], F32, name=f"bank{((0, 1, 2, 3), (0, 1, 2, 4))[c][t]}")
             col = a * H + t * P
             plane = vs[c][:] if a == 0 else vs1[:, c * CH:(c + 1) * CH]
             nc.tensor.matmul_mx(
@@ -223,8 +213,9 @@ def tile_list_spectrum_probe_contrast_kernel(
             nc.scalar.activation(out=roots[c, t][:], in_=mags[c, t][:], func=ACT.Abs_reciprocal_sqrt, bias=lev[:, t:t + 1])
 
         def square(c, t):
-            if (c, t) == (0, PACK - 1):
-                recip[c, t, 0] = turns.tile([P, CH], F32, name="recip0_3", align_bytes=64, offset=13312)
+            if (c, t) in ((0, 3), (1, 1), (1, 2)):
+                at = {(0, 3): 13312, (1, 1): 40960, (1, 2): 47104}[c, t]
+                recip[c, t, 0] = turns.tile([P, CH], F32, name=f"recip{c}_{t}", align_bytes=64, offset=at)
             else:
                 recip[c, t, 0] = keep.tile([P, CH], F32, name=f"recip{c}_{t}", tag=f"recip{c}_{t}", align_bytes=64)
             nc.scalar.activation(out=recip[c, t, 0][:], in_=roots[c, t][:], func=ACT.Square)
@@ -236,7 +227,7 @@ def tile_list_spectrum_probe_contrast_kernel(
                 if t > 0:
                     square(c, t - 1)
 
-        w8p = keep.tile([P, PASSES * H], I32, name="w8p", align_bytes=64)
+        w8p = [keep.tile([P, H], I32, name=f"w8p{a}", align_bytes=64) for a in range(PASSES)]
         hs = [
             keep.tile([P, PACK, CH], F32, name="h0", align_bytes=64),
             turns.tile([P, PACK, CH], F32, name="h1", align_bytes=64, offset=23552),
@@ -257,15 +248,17 @@ def tile_list_spectrum_probe_contrast_kernel(
             diff[c, t] = psum.tile([P, CH], F32, name=f"bank{bank}")
             w1_pass(c, t, a, True, False)
 
-        def w8_passes(c, t, start=False):
+        def w8_pass(c, t, a, start=False):
+            nc.tensor.matmul_mx(
+                out=diff[c, t][:],
+                lhsT=w8p[a][:, t * P:(t + 1) * P].bitcast(FP8X4), lhsT_scale=w8scp[4 * a:, t * P:(t + 1) * P],
+                rhs=vw[a][c][:].bitcast(FP8X4), rhs_scale=vscale(a, c),
+                start=start, stop=False,
+            )
+
+        def w8_passes(c, t):
             for a in range(PASSES):
-                col = a * H + t * P
-                nc.tensor.matmul_mx(
-                    out=diff[c, t][:],
-                    lhsT=w8p[:, col:col + P].bitcast(FP8X4), lhsT_scale=w8scp[4 * a:, t * P:(t + 1) * P],
-                    rhs=vw[a][c][:].bitcast(FP8X4), rhs_scale=vscale(a, c),
-                    start=(start and a == 0), stop=False,
-                )
+                w8_pass(c, t, a)
 
         def contrast(c, t, lo=0, hi=CH):
             nc.vector.scalar_tensor_tensor(hs[c][:, t, lo:hi], diff[c, t][:, lo:hi], -1.0, recip[c, t, lo][:], ALU.mult, ALU.mult)
@@ -374,7 +367,7 @@ def tile_list_spectrum_probe_contrast_kernel(
         inverse_root(0, 1)
         magnitude(0, 3)
         gather(1, 1)
-        for t in range(2):
+        for t in range(PACK - 1):
             both_pass(1, t, 1, 1)
             both_pass(1, t, 0, 1)
         square(0, 0)
@@ -387,16 +380,18 @@ def tile_list_spectrum_probe_contrast_kernel(
         magnitude(1, 1)
         inverse_root(1, 0)
         cast_w1(0, False)
-        deal_w8()
+        deal_w8(0)
+        deal_w8_scales()
         quant_w1(0)
         for t in range(PACK - 1):
             diff[0, t] = psum.tile([P, CH], F32, name=f"bank{4 + t}")
-            w8_passes(0, t, True)
+            w8_pass(0, t, 0, True)
             w1_pass(0, t, 0, False, False)
-        cast_w1_half(0)
-        cast_w1_half(1)
+        cast_w1(1, False)
+        deal_w8(1)
         quant_w1(1)
         for t in range(PACK - 1):
+            w8_pass(0, t, 1)
             w1_pass(0, t, 1, False, True)
         open_diff(0, PACK - 1, 7, 1)
         w8_passes(0, PACK - 1)
@@ -405,9 +400,8 @@ def tile_list_spectrum_probe_contrast_kernel(
         cast_rows_gpsimd(wrbfa[:], wrraw[0], 0, 256)
         for t in range(PACK):
             contrast(0, t)
-        for t in range(2, PACK):
-            both_pass(1, t, 1, 1)
-            both_pass(1, t, 0, 1)
+        both_pass(1, PACK - 1, 1, 1)
+        both_pass(1, PACK - 1, 0, 1)
         magnitude(1, 2)
         inverse_root(1, 1)
         magnitude(1, 3)
@@ -427,9 +421,10 @@ def tile_list_spectrum_probe_contrast_kernel(
         quant_h(0)
         quant_o(wrbf1, N, 0, 256)
         quant_o(wrbf1, N, 256, 384)
-        wgbf = turns.tile([P, N * PACK], BF16, name="wgbf", align_bytes=64, offset=11264)
-        cast_rows_gpsimd(wgbf[:, :WG_SPLIT * PACK], wgraw, 0, WG_SPLIT)
-        cast_rows(wgbf[:, WG_SPLIT * PACK:], wgraw, nc.scalar.copy, WG_SPLIT, N)
+        wgbf = turns.tile([P, WG_SPLIT * PACK], BF16, name="wgbf", align_bytes=64, offset=11264)
+        wgbfb = keep.tile([P, (N - WG_SPLIT) * PACK], BF16, name="wgbfb", align_bytes=64)
+        cast_rows_gpsimd(wgbf[:], wgraw, 0, WG_SPLIT)
+        cast_rows(wgbfb[:], wgraw, nc.scalar.copy, WG_SPLIT, N)
         warm3 = keep.tile([P, 1], F32, name="warm3")
         nc.scalar.activation(out=warm3[:], in_=recip[1, PACK - 1, 0][:, 0:1], func=ACT.Sigmoid)
         for t in range(PACK):
@@ -441,7 +436,8 @@ def tile_list_spectrum_probe_contrast_kernel(
             raw_product(0, j, 2 + j)
         raw_product(1, 0, 5)
         quant_o(wgbf, 768, 0, 256)
-        quant_o(wgbf, 768, 256, 384)
+        quant_o(wgbf, 768, 256, WG_SPLIT)
+        quant_o(wgbfb, 768, WG_SPLIT, N, True)
         cast_h(1, 0, SPLIT)
         cast_h(1, SPLIT, CH, nc.scalar.copy)
         for j in range(NT):

@@ -24,8 +24,6 @@ CH = 512
 CHUNKS = S // CH
 NT = N // P
 HALF = CH // 2
-SPLIT = 288
-WG_SPLIT = 320
 
 
 def tile_list_spectrum_probe_contrast_kernel(
@@ -172,7 +170,7 @@ def tile_list_spectrum_probe_contrast_kernel(
 
         def both_pass(c, t, a, first=0):
             if a == first:
-                sums[c, t] = psum.tile([P, CH], F32, name=f"bank{((0, 1, 2, 3), (0, 1, 2, 4))[c][t]}")
+                sums[c, t] = psum.tile([P, CH], F32, name=f"bank{((0, 1, 2, 3), (0, 1, 4, 5))[c][t]}")
             col = a * H + t * P
             plane = vs[c][:] if a == 0 else vs1[:, c * CH:(c + 1) * CH]
             nc.tensor.matmul_mx(
@@ -304,9 +302,7 @@ def tile_list_spectrum_probe_contrast_kernel(
         def quant_h(c, lo=0, hi=CH):
             cols = slice(c * CH + lo, c * CH + hi)
             nc.vector.quantize_mx(out=hq[:, cols].bitcast(FP8X4), scales=hsc[:, cols], in_=hbf[c][:, PACK * lo:PACK * hi])
-            if hi == CH:
-                whole = slice(c * CH, (c + 1) * CH)
-                nc.sync.dma_start(out2v[:, whole], hq[:, whole].bitcast(I32))
+            nc.sync.dma_start(out2v[:, cols], hq[:, cols].bitcast(I32))
 
         def pieces(c, j):
             if (c, j) == (CHUNKS - 1, NT - 1):
@@ -367,7 +363,7 @@ def tile_list_spectrum_probe_contrast_kernel(
         inverse_root(0, 1)
         magnitude(0, 3)
         gather(1, 1)
-        for t in range(PACK - 1):
+        for t in range(2):
             both_pass(1, t, 1, 1)
             both_pass(1, t, 0, 1)
         square(0, 0)
@@ -383,25 +379,23 @@ def tile_list_spectrum_probe_contrast_kernel(
         deal_w8(0)
         deal_w8_scales()
         quant_w1(0)
-        for t in range(PACK - 1):
+        for t in range(PACK):
             diff[0, t] = psum.tile([P, CH], F32, name=f"bank{4 + t}")
             w8_pass(0, t, 0, True)
             w1_pass(0, t, 0, False, False)
         cast_w1(1, False)
         deal_w8(1)
         quant_w1(1)
-        for t in range(PACK - 1):
+        for t in range(PACK):
             w8_pass(0, t, 1)
             w1_pass(0, t, 1, False, True)
-        open_diff(0, PACK - 1, 7, 1)
-        w8_passes(0, PACK - 1)
-        w1_pass(0, PACK - 1, 0, False, True)
         wrbfa = turns.tile([P, 256 * PACK], BF16, name="wrbfa", align_bytes=64, offset=24576)
         cast_rows_gpsimd(wrbfa[:], wrraw[0], 0, 256)
         for t in range(PACK):
             contrast(0, t)
-        both_pass(1, PACK - 1, 1, 1)
-        both_pass(1, PACK - 1, 0, 1)
+        for t in range(2, PACK):
+            both_pass(1, t, 1, 1)
+            both_pass(1, t, 0, 1)
         magnitude(1, 2)
         inverse_root(1, 1)
         magnitude(1, 3)
@@ -421,10 +415,8 @@ def tile_list_spectrum_probe_contrast_kernel(
         quant_h(0)
         quant_o(wrbf1, N, 0, 256)
         quant_o(wrbf1, N, 256, 384)
-        wgbf = turns.tile([P, WG_SPLIT * PACK], BF16, name="wgbf", align_bytes=64, offset=11264)
-        wgbfb = keep.tile([P, (N - WG_SPLIT) * PACK], BF16, name="wgbfb", align_bytes=64)
-        cast_rows_gpsimd(wgbf[:], wgraw, 0, WG_SPLIT)
-        cast_rows(wgbfb[:], wgraw, nc.scalar.copy, WG_SPLIT, N)
+        wgbf = turns.tile([P, N * PACK], BF16, name="wgbf", align_bytes=64, offset=11264)
+        cast_rows_gpsimd(wgbf[:], wgraw, 0, N)
         warm3 = keep.tile([P, 1], F32, name="warm3")
         nc.scalar.activation(out=warm3[:], in_=recip[1, PACK - 1, 0][:, 0:1], func=ACT.Sigmoid)
         for t in range(PACK):
@@ -434,23 +426,23 @@ def tile_list_spectrum_probe_contrast_kernel(
             contrast(1, t)
         for j in range(NT):
             raw_product(0, j, 2 + j)
-        raw_product(1, 0, 5)
         quant_o(wgbf, 768, 0, 256)
-        quant_o(wgbf, 768, 256, WG_SPLIT)
-        quant_o(wgbfb, 768, WG_SPLIT, N, True)
-        cast_h(1, 0, SPLIT)
-        cast_h(1, SPLIT, CH, nc.scalar.copy)
+        quant_o(wgbf, 768, 256, N)
+        cast_h(1, 0, HALF)
+        cast_h(1, HALF, CH, nc.scalar.copy)
         for j in range(NT):
-            readout(0, j, (0, 1, 6)[j])
-        quant_h(1)
+            readout(0, j, (0, 1, 5)[j])
+        quant_h(1, 0, HALF)
+        quant_h(1, HALF, CH)
         for q in range(4):
             nc.sync.dma_start(out_3[0, 4 * q:4 * q + 4, :].bitcast(I32), hsc[32 * q:32 * q + 4, :].bitcast(I32))
         for j in range(NT):
             finish(0, j)
-        raw_product(1, 1, 0)
-        readout(1, 0, 7)
-        readout(1, 1, 1)
-        raw_product(1, 2, 6)
-        readout(1, 2, 2)
+        readout(1, 0, 6)
+        readout(1, 1, 7)
+        raw_product(1, 0, 0)
+        raw_product(1, 1, 1)
+        readout(1, 2, 5)
+        raw_product(1, 2, 2)
         for j in range(NT):
             finish(1, j)

@@ -145,7 +145,7 @@ def tile_list_spectrum_probe_contrast_kernel(
             cols = slice((c * CH + lo) // 16, (c * CH + hi) // 16)
             nc.vector.tensor_copy(vw[a][c][:, lo:hi], tabw[a][:].bitcast(U32).indirect(offsets[:, cols]))
 
-        w1bf = [turns.tile([P, PACK * H], BF16, name=f"w1bf{a}", align_bytes=64, offset=(8192, 24576)[a]) for a in range(PASSES)]
+        w1bf = [turns.tile([P, PACK * H], BF16, name=f"w1bf{a}", align_bytes=64, offset=(0, 24576)[a]) for a in range(PASSES)]
         w1q = [keep.tile([P, H], U32, name=f"w1q{a}", align_bytes=64) for a in range(PASSES)]
         w1s = [keep.tile([P, H], U8, name=f"w1s{a}", align_bytes=64) for a in range(PASSES)]
 
@@ -211,8 +211,8 @@ def tile_list_spectrum_probe_contrast_kernel(
             nc.scalar.activation(out=roots[c, t][:], in_=mags[c, t][:], func=ACT.Abs_reciprocal_sqrt, bias=lev[:, t:t + 1])
 
         def square(c, t):
-            if (c, t) in ((0, 3), (1, 1), (1, 2)):
-                at = {(0, 3): 13312, (1, 1): 40960, (1, 2): 47104}[c, t]
+            if (c, t) in ((0, 2), (1, 1), (1, 2)):
+                at = {(0, 2): 13312, (1, 1): 40960, (1, 2): 47104}[c, t]
                 recip[c, t, 0] = turns.tile([P, CH], F32, name=f"recip{c}_{t}", align_bytes=64, offset=at)
             else:
                 recip[c, t, 0] = keep.tile([P, CH], F32, name=f"recip{c}_{t}", tag=f"recip{c}_{t}", align_bytes=64)
@@ -415,8 +415,8 @@ def tile_list_spectrum_probe_contrast_kernel(
         quant_h(0)
         quant_o(wrbf1, N, 0, 256)
         quant_o(wrbf1, N, 256, 384)
-        wgbf = turns.tile([P, N * PACK], BF16, name="wgbf", align_bytes=64, offset=11264)
-        cast_rows_gpsimd(wgbf[:], wgraw, 0, N)
+        wgbf = turns.tile([P, 256 * PACK], BF16, name="wgbf", align_bytes=64, offset=11264)
+        cast_rows_gpsimd(wgbf[:], wgraw, 0, 256)
         warm3 = keep.tile([P, 1], F32, name="warm3")
         nc.scalar.activation(out=warm3[:], in_=recip[1, PACK - 1, 0][:, 0:1], func=ACT.Sigmoid)
         for t in range(PACK):
@@ -427,8 +427,10 @@ def tile_list_spectrum_probe_contrast_kernel(
         for j in range(NT):
             raw_product(0, j, 2 + j)
         quant_o(wgbf, 768, 0, 256)
-        quant_o(wgbf, 768, 256, N)
+        wgbfb = keep.tile([P, 128 * PACK], BF16, name="wgbfb", tag="recip1_3", align_bytes=64)
+        cast_rows(wgbfb[:], wgraw, nc.vector.tensor_copy, 256, N)
         cast_h(1, 0, HALF)
+        quant_o(wgbfb, 768, 256, N, True)
         cast_h(1, HALF, CH, nc.scalar.copy)
         for j in range(NT):
             readout(0, j, (0, 1, 5)[j])

from contextlib import ExitStack

import concourse.mybir as mybir

K, T, S, H, N = 1024, 2048, 1024, 512, 384
FLOPS = 2 * S * (3 * K * H + K * N + H * N)

F32 = mybir.dt.float32
BF16 = mybir.dt.bfloat16
I32 = mybir.dt.int32
U32 = mybir.dt.uint32
U16 = mybir.dt.uint16
U8 = mybir.dt.uint8
FP8X4 = mybir.dt.float8_e4m3fn_x4
FP4X4 = mybir.dt.float4_e2m1fn_x4
ACT = mybir.ActivationFunctionType
ALU = mybir.AluOpType

P = 128
PACK = 4
KP = P * PACK
PASSES = K // KP
CH = 512
CHUNKS = S // CH
NT = N // P
HALF = CH // 2


def tile_list_spectrum_probe_contrast_kernel(
    tc, tab_words, tab_scales, offs, w1, w8_words, w8_scales, w4_words, w4_scales, level, wg, wr,
    out_0, out_1, out_2, out_3,
):
    nc = tc.nc
    with ExitStack() as ctx:
        keep = ctx.enter_context(tc.tile_pool(name="keep", bufs=1))
        turns = ctx.enter_context(tc.tile_pool(name="turns", bufs=1))
        ring = ctx.enter_context(tc.tile_pool(name="ring", bufs=3))
        psum = ctx.enter_context(tc.psum_pool(name="psum", bufs=1))

        offsets = keep.tile([P, S // 16], U16, name="offsets")
        tsc_tile = keep.tile([P, T], U8, name="tsc", align_bytes=64)
        tsc = tsc_tile[:]
        wsc = keep.tile([P, PASSES * H], U8, name="wsc", tag="wsc", align_bytes=64)
        vs1 = keep.tile([P, S], U8, name="vs1", align_bytes=64)
        warm = keep.tile([P, 1], F32, name="warm")
        warm2 = keep.tile([P, 1], F32, name="warm2")
        w8sc = keep.tile([P, H], U8, name="w8sc", align_bytes=64)
        vs = [
            keep.tile([P, CH], U8, name="gsc0", align_bytes=64),
            keep.tile([P, CH], U8, name="gsc1", align_bytes=64),
        ]
        nc.vector.memset(tsc.bitcast(I32), 0)
        nc.gpsimd.memset(w8sc[:].bitcast(I32), 0)
        nc.vector.memset(warm[:], 1.0)
        nc.vector.memset(wsc[:].bitcast(I32), 0)
        nc.vector.memset(vs1[:].bitcast(I32), 0)
        nc.scalar.activation(out=warm2[:], in_=warm[:], func=ACT.Abs_reciprocal_sqrt)

        nc.sync.dma_start(offsets[:], offs)
        tabw = [turns.tile([P, T], I32, name=f"tabw{a}", align_bytes=64, offset=(0, 8192)[a]) for a in range(PASSES)]
        w1raw = [turns.tile([P, PACK * H], F32, name=f"w1raw{a}", align_bytes=64, offset=(24576, 32768)[a]) for a in range(PASSES)]
        wrraw = [turns.tile([P, PACK * N], F32, name=f"wrraw{a}", align_bytes=64, offset=(40960, 47104)[a]) for a in range(PASSES)]
        wgraw = turns.tile([P, PACK * N], F32, name="wgraw", align_bytes=64, offset=53248)
        w4raw = keep.tile([P, PASSES * 2 * H], U8, name="w4raw", align_bytes=64)
        w8raw = [keep.tile([P, H], I32, name=f"w8raw{a}", align_bytes=64) for a in range(PASSES)]
        lev = keep.tile([P, PACK], F32, name="lev")

        def load_tab(a):
            nc.sync.dma_start(tabw[a][:], tab_words[a].rearrange("p t i -> p (t i)").bitcast(I32))

        def load_rows(dst, src, a, queue=nc.sync):
            queue.dma_start(dst[:], src[a * KP:(a + 1) * KP, :].rearrange("(p j) c -> p (j c)", j=PACK))

        def load_wscales(eng, src, row0):
            for q in range(4):
                eng.dma_start(
                    wsc[32 * q + row0:32 * q + row0 + 4, :].bitcast(I32).rearrange("r (a c) -> r a c", a=PASSES),
                    src[:, 4 * q:4 * q + 4, :].bitcast(I32).rearrange("a r c -> r a c"),
                )

        nc.sync.dma_start(
            w4raw[:].bitcast(I32).rearrange("p (a c) -> p a c", a=PASSES),
            w4_words.bitcast(I32).rearrange("a p c -> p a c"),
        )
        for r in range(4):
            nc.sync.dma_start(
                tsc_tile[r:P:16, :].bitcast(I32),
                tab_scales.bitcast(I32).rearrange("a (q r) c -> r q a c", r=4)[r],
            )
        for q in range(4):
            nc.gpsimd.dma_start(w8sc[32 * q:32 * q + 8, :].bitcast(I32), w8_scales[:, 4 * q:4 * q + 4, :].bitcast(I32))
        load_tab(0)
        load_wscales(nc.sync, w4_scales, 0)
        load_tab(1)
        nc.sync.dma_start(lev[:], level.rearrange("(p t) -> p t", t=PACK))

        w4p = keep.tile([P, PASSES * 2 * H], U8, name="w4p", align_bytes=64)
        nc.vector.tensor_copy(
            w4p[:].bitcast(U16).rearrange("p (a t m) -> p a t m", a=PASSES, t=PACK),
            w4raw[:].bitcast(U16).rearrange("p (a m t) -> p a t m", a=PASSES, t=PACK),
        )
        def gather_scales(c):
            nc.vector.tensor_copy(vs[c][:], tsc.indirect(offsets[:, c * (CH // 16):(c + 1) * (CH // 16)]))
            nc.scalar.dma_start(vs1[0:112, c * CH:(c + 1) * CH].bitcast(I32), vs[c][16:128, :].bitcast(I32))

        gather_scales(0)
        gather_scales(1)
        load_rows(w1raw[0], w1, 0)
        nc.sync.dma_start(w8raw[0][:], w8_words[0].rearrange("p c i -> p (c i)").bitcast(I32))
        load_rows(w1raw[1], w1, 1)
        nc.sync.dma_start(w8raw[1][:], w8_words[1].rearrange("p c i -> p (c i)").bitcast(I32))
        load_rows(wrraw[0], wr, 0)
        load_rows(wrraw[1], wr, 1)
        load_rows(wgraw, wg, 0)
        wscp = keep.tile([P, PASSES * H], U8, name="wscp", align_bytes=64)
        w8scp = keep.tile([P, H], U8, name="w8scp", tag="wsc", align_bytes=64)

        def deal_w4_scales():
            for a in range(PASSES):
                nc.gpsimd.tensor_copy(
                    wscp[:, a * H:(a + 1) * H].rearrange("p (t m) -> p t m", t=PACK),
                    wsc[:, a * H:(a + 1) * H].rearrange("p (m t) -> p t m", t=PACK),
                )

        def deal_w8(a):
            nc.vector.tensor_copy(
                w8p[a][:].rearrange("p (t m) -> p m t", t=PACK),
                w8raw[a][:].rearrange("p (m t) -> p m t", t=PACK),
            )

        def deal_w8_scales():
            nc.gpsimd.tensor_copy(
                w8scp[:].rearrange("p (t m) -> p t m", t=PACK),
                w8sc[:].rearrange("p (m t) -> p t m", t=PACK),
            )

        vw = [
            [keep.tile([P, CH], U32, name="vw0_0", align_bytes=64),
             keep.tile([P, CH], U32, name="vw0_1", align_bytes=64)],
            [keep.tile([P, CH], U32, name="vw1_0", align_bytes=64),
             keep.tile([P, CH], U32, name="vw1_1", align_bytes=64)],
        ]

        def gather(a, c, lo=0, hi=CH):
            cols = slice((c * CH + lo) // 16, (c * CH + hi) // 16)
            nc.vector.tensor_copy(vw[a][c][:, lo:hi], tabw[a][:].bitcast(U32).indirect(offsets[:, cols]))

        w1bf = [turns.tile([P, PACK * H], BF16, name=f"w1bf{a}", align_bytes=64, offset=(0, 24576)[a]) for a in range(PASSES)]
        w1q = [keep.tile([P, H], U32, name=f"w1q{a}", align_bytes=64) for a in range(PASSES)]
        w1s = [keep.tile([P, H], U8, name=f"w1s{a}", align_bytes=64) for a in range(PASSES)]

        def cast_w1(a, on_scalar):
            dst = w1bf[a][:].rearrange("p (t m j) -> p m j t", t=PACK, j=PACK)
            src = w1raw[a][:].rearrange("p (j m t) -> p m j t", t=PACK, j=PACK)
            if on_scalar:
                nc.scalar.activation(out=dst, in_=src, func=ACT.Copy, scale=-1.0)
            else:
                nc.vector.tensor_scalar(dst, src, -1.0, None, ALU.mult)

        def quant_w1(a):
            nc.vector.quantize_mx(out=w1q[a][:].bitcast(FP8X4), scales=w1s[a][:], in_=w1bf[a][:])

        def vscale(a, c):
            return vs[c][:] if a == 0 else vs1[:, c * CH:(c + 1) * CH]

        recip = {}
        mags = {}

        sums = {}

        def both_pass(c, t, a, first=0):
            if a == first:
                sums[c, t] = psum.tile([P, CH], F32, name=f"bank{((0, 1, 2, 3), (0, 1, 4, 5))[c][t]}")
            col = a * H + t * P
            plane = vs[c][:] if a == 0 else vs1[:, c * CH:(c + 1) * CH]
            nc.tensor.matmul_mx(
                out=sums[c, t][:],
                lhsT=w4p[:, 2 * col:2 * (col + P)].bitcast(FP4X4), lhsT_scale=wscp[:, col:col + P],
                rhs=vw[a][c][:].bitcast(FP8X4), rhs_scale=plane,
                start=(a == first), stop=(a != first),
            )

        halves = {}

        def half_pass(t, u, a):
            if a == 0:
                halves[t, u] = psum.tile([P, CH], F32, name=f"bank{t + 4 * (1 - u)}")
            col = a * H + t * P
            for i in range(2):
                cols = slice(u * HALF + i * P, u * HALF + (i + 1) * P)
                nc.tensor.matmul_mx(
                    out=halves[t, u][:, i * P:(i + 1) * P],
                    lhsT=w4p[:, 2 * col:2 * (col + P)].bitcast(FP4X4), lhsT_scale=wscp[:, col:col + P],
                    rhs=vw[a][0][:, cols].bitcast(FP8X4), rhs_scale=vscale(a, 0)[:, cols],
                    start=(a == 0 and i == 0), stop=(a == 1 and i == 1),
                )

        def half_magnitude(t, u):
            if u == 0:
                mags[0, t] = keep.tile([P, CH], F32, name=f"mag0_{t}", tag=f"mag0_{t}", align_bytes=64)
            nc.scalar.activation(out=mags[0, t][:, u * HALF:(u + 1) * HALF], in_=halves[t, u][:, 0:HALF], func=ACT.Abs)

        def magnitude(c, t):
            mags[c, t] = keep.tile([P, CH], F32, name=f"mag{c}_{t}", tag=f"mag{c}_{t}", align_bytes=64)
            nc.scalar.activation(out=mags[c, t][:], in_=sums[c, t][:], func=ACT.Abs)

        roots = {}

        def inverse_root(c, t):
            roots[c, t] = ring.tile([P, CH], F32, name="root")
            nc.scalar.activation(out=roots[c, t][:], in_=mags[c, t][:], func=ACT.Abs_reciprocal_sqrt, bias=lev[:, t:t + 1])

        def square(c, t):
            if (c, t) in ((0, 2), (1, 1), (1, 2)):
                at = {(0, 2): 13312, (1, 1): 40960, (1, 2): 47104}[c, t]
                recip[c, t, 0] = turns.tile([P, CH], F32, name=f"recip{c}_{t}", align_bytes=64, offset=at)
            else:
                recip[c, t, 0] = keep.tile([P, CH], F32, name=f"recip{c}_{t}", tag=f"recip{c}_{t}", align_bytes=64)
            nc.scalar.activation(out=recip[c, t, 0][:], in_=roots[c, t][:], func=ACT.Square)

        def invert_all(c):
            for t in range(PACK + 1):
                if t < PACK:
                    inverse_root(c, t)
                if t > 0:
                    square(c, t - 1)

        w8p = [keep.tile([P, H], I32, name=f"w8p{a}", align_bytes=64) for a in range(PASSES)]
        hs = [
            keep.tile([P, PACK, CH], F32, name="h0", align_bytes=64),
            turns.tile([P, PACK, CH], F32, name="h1", align_bytes=64, offset=23552),
        ]
        out1v = out_1.rearrange("(p t) s -> p t s", t=PACK)

        diff = {}

        def w1_pass(c, t, a, start, stop):
            nc.tensor.matmul_mx(
                out=diff[c, t][:],
                lhsT=w1q[a][:, t * P:(t + 1) * P].bitcast(FP8X4), lhsT_scale=w1s[a][:, t * P:(t + 1) * P],
                rhs=vw[a][c][:].bitcast(FP8X4), rhs_scale=vscale(a, c),
                start=start, stop=stop,
            )

        def open_diff(c, t, bank, a):
            diff[c, t] = psum.tile([P, CH], F32, name=f"bank{bank}")
            w1_pass(c, t, a, True, False)

        def w8_pass(c, t, a, start=False):
            nc.tensor.matmul_mx(
                out=diff[c, t][:],
                lhsT=w8p[a][:, t * P:(t + 1) * P].bitcast(FP8X4), lhsT_scale=w8scp[4 * a:, t * P:(t + 1) * P],
                rhs=vw[a][c][:].bitcast(FP8X4), rhs_scale=vscale(a, c),
                start=start, stop=False,
            )

        def w8_passes(c, t):
            for a in range(PASSES):
                w8_pass(c, t, a)

        def contrast(c, t, lo=0, hi=CH):
            nc.vector.scalar_tensor_tensor(hs[c][:, t, lo:hi], diff[c, t][:, lo:hi], -1.0, recip[c, t, lo][:], ALU.mult, ALU.mult)
            if hi == CH:
                nc.sync.dma_start(out1v[:, t, c * CH:(c + 1) * CH], hs[c][:, t, :])

        oq = keep.tile([P, (PASSES + 1) * N], U32, name="oq", align_bytes=64)
        osc = keep.tile([P, (PASSES + 1) * N], U8, name="osc", align_bytes=64)

        def cast_rows(dst, src, copy=nc.vector.tensor_copy, lo=0, hi=N):
            copy(
                dst.rearrange("p (c i j) -> p c j i", i=4, j=PACK),
                src[:].rearrange("p (j c) -> p j c", j=PACK)[:, :, lo:hi].rearrange("p j (c i) -> p c j i", i=4),
            )

        def cast_rows_gpsimd(dst, src, lo, hi):
            nc.gpsimd.tensor_scalar(
                dst.rearrange("p (c j) -> p c j", j=PACK),
                src[:].rearrange("p (j c) -> p c j", j=PACK)[:, lo:hi, :],
                1.0, 0.0, ALU.mult, ALU.add,
            )

        def quant_o(src, col0, lo, hi, whole=False):
            cols = slice(col0 + lo, col0 + hi)
            part = src[:] if whole else src[:, PACK * lo:PACK * hi]
            nc.vector.quantize_mx(out=oq[:, cols].bitcast(FP8X4), scales=osc[:, cols], in_=part)

        hq = keep.tile([P, S], U32, name="hq", align_bytes=64)
        hsc = keep.tile([P, S], U8, name="hsc", align_bytes=64)
        out2v = out_2[0].rearrange("p s i -> p (s i)").bitcast(I32)

        hbf = [
            turns.tile([P, CH * PACK], BF16, name="hbf0", align_bytes=64, offset=20480),
            keep.tile([P, CH * PACK], BF16, name="hbf1", align_bytes=64),
        ]

        def cast_h(c, lo=0, hi=CH, copy=nc.vector.tensor_copy):
            copy(
                hbf[c][:, PACK * lo:PACK * hi].rearrange("p (c i t) -> p c t i", i=4, t=PACK),
                hs[c][:, :, lo:hi].rearrange("p t (c i) -> p c t i", i=4),
            )

        def quant_h(c, lo=0, hi=CH):
            cols = slice(c * CH + lo, c * CH + hi)
            nc.vector.quantize_mx(out=hq[:, cols].bitcast(FP8X4), scales=hsc[:, cols], in_=hbf[c][:, PACK * lo:PACK * hi])
            nc.sync.dma_start(out2v[:, cols], hq[:, cols].bitcast(I32))

        def pieces(c, j):
            if (c, j) == (CHUNKS - 1, NT - 1):
                return ((0, HALF), (HALF, CH))
            return ((0, CH),)

        raws = {}
        sigs = {}

        def raw_product(c, j, bank):
            raws[c, j] = psum.tile([P, CH], F32, name=f"bank{bank}")
            for a in range(PASSES):
                col = a * N + j * P
                nc.tensor.matmul_mx(
                    out=raws[c, j][:],
                    lhsT=oq[:, col:col + P].bitcast(FP8X4), lhsT_scale=osc[:, col:col + P],
                    rhs=vw[a][c][:].bitcast(FP8X4), rhs_scale=vscale(a, c),
                    start=(a == 0), stop=(a == PASSES - 1),
                )

        def readout(c, j, bank):
            cols = slice(c * CH, (c + 1) * CH)
            gate = psum.tile([P, CH], F32, name=f"bank{bank}")
            col = PASSES * N + j * P
            nc.tensor.matmul_mx(
                out=gate[:],
                lhsT=oq[:, col:col + P].bitcast(FP8X4), lhsT_scale=osc[:, col:col + P],
                rhs=hq[:, cols].bitcast(FP8X4), rhs_scale=hsc[:, cols],
                start=True, stop=True,
            )
            sigs[c, j] = keep.tile([P, CH], F32, name=f"sig{c}_{j}")
            for lo, hi in pieces(c, j):
                nc.scalar.activation(out=sigs[c, j][:, lo:hi], in_=gate[:, lo:hi], func=ACT.Sigmoid)

        def finish(c, j):
            y = keep.tile([P, CH], F32, name=f"y{c}_{j}")
            for lo, hi in pieces(c, j):
                nc.vector.tensor_tensor(y[:, lo:hi], raws[c, j][:, lo:hi], sigs[c, j][:, lo:hi], ALU.mult)
                nc.sync.dma_start(out_0[j * P:(j + 1) * P, c * CH + lo:c * CH + hi], y[:, lo:hi])

        gather(0, 0, 0, HALF)
        gather(0, 0, HALF, CH)
        deal_w4_scales()
        gather(0, 1)
        gather(1, 0, 0, HALF)
        gather(1, 0, HALF, CH)
        for a in range(PASSES):
            for u in range(2):
                for t in range(2):
                    half_pass(t, u, a)
            for t in range(2, PACK):
                both_pass(0, t, a)
        for u in range(2):
            for t in range(2):
                half_magnitude(t, u)
        inverse_root(0, 0)
        magnitude(0, 2)
        inverse_root(0, 1)
        magnitude(0, 3)
        gather(1, 1)
        for t in range(2):
            both_pass(1, t, 1, 1)
            both_pass(1, t, 0, 1)
        square(0, 0)
        inverse_root(0, 2)
        square(0, 1)
        inverse_root(0, 3)
        square(0, 2)
        square(0, 3)
        magnitude(1, 0)
        magnitude(1, 1)
        inverse_root(1, 0)
        cast_w1(0, False)
        deal_w8(0)
        deal_w8_scales()
        quant_w1(0)
        for t in range(PACK):
            diff[0, t] = psum.tile([P, CH], F32, name=f"bank{4 + t}")
            w8_pass(0, t, 0, True)
            w1_pass(0, t, 0, False, False)
        cast_w1(1, False)
        deal_w8(1)
        quant_w1(1)
        for t in range(PACK):
            w8_pass(0, t, 1)
            w1_pass(0, t, 1, False, True)
        wrbfa = turns.tile([P, 256 * PACK], BF16, name="wrbfa", align_bytes=64, offset=24576)
        cast_rows_gpsimd(wrbfa[:], wrraw[0], 0, 256)
        for t in range(PACK):
            contrast(0, t)
        for t in range(2, PACK):
            both_pass(1, t, 1, 1)
            both_pass(1, t, 0, 1)
        magnitude(1, 2)
        inverse_root(1, 1)
        magnitude(1, 3)
        square(1, 0)
        inverse_root(1, 2)
        square(1, 1)
        inverse_root(1, 3)
        square(1, 2)
        square(1, 3)
        wrbfb = turns.tile([P, 128 * PACK], BF16, name="wrbfb", align_bytes=64, offset=14336)
        cast_rows(wrbfb[:], wrraw[0], nc.vector.tensor_copy, 256, 384)
        wrbf1 = turns.tile([P, N * PACK], BF16, name="wrbf1", align_bytes=64, offset=11264)
        cast_rows(wrbf1[:], wrraw[1])
        cast_h(0)
        quant_o(wrbfa, 0, 0, 256, True)
        quant_o(wrbfb, 0, 256, 384, True)
        quant_h(0)
        quant_o(wrbf1, N, 0, 256)
        quant_o(wrbf1, N, 256, 384)
        wgbf = turns.tile([P, 256 * PACK], BF16, name="wgbf", align_bytes=64, offset=11264)
        cast_rows_gpsimd(wgbf[:], wgraw, 0, 256)
        warm3 = keep.tile([P, 1], F32, name="warm3")
        nc.scalar.activation(out=warm3[:], in_=recip[1, PACK - 1, 0][:, 0:1], func=ACT.Sigmoid)
        for t in range(PACK):
            open_diff(1, t, (0, 1, 6, 7)[t], 1)
            w8_passes(1, t)
            w1_pass(1, t, 0, False, True)
            contrast(1, t)
        for j in range(NT):
            raw_product(0, j, 2 + j)
        quant_o(wgbf, 768, 0, 256)
        wgbfb = keep.tile([P, 128 * PACK], BF16, name="wgbfb", tag="recip1_3", align_bytes=64)
        cast_rows(wgbfb[:], wgraw, nc.vector.tensor_copy, 256, N)
        cast_h(1, 0, HALF)
        quant_o(wgbfb, 768, 256, N, True)
        cast_h(1, HALF, CH, nc.scalar.copy)
        for j in range(NT):
            readout(0, j, (0, 1, 5)[j])
        quant_h(1, 0, HALF)
        quant_h(1, HALF, CH)
        for q in range(4):
            nc.sync.dma_start(out_3[0, 4 * q:4 * q + 4, :].bitcast(I32), hsc[32 * q:32 * q + 4, :].bitcast(I32))
        for j in range(NT):
            finish(0, j)
        readout(1, 0, 6)
        readout(1, 1, 7)
        raw_product(1, 0, 0)
        raw_product(1, 1, 1)
        readout(1, 2, 5)
        raw_product(1, 2, 2)
        for j in range(NT):
            finish(1, j)
